import numpy as np
import ml_dtypes


def mxq(x, axis, fmt="e4m3"):
    dtype, down = {"e4m3": (ml_dtypes.float8_e4m3fn, 7), "e5m2": (ml_dtypes.float8_e5m2, 14)}[fmt]
    v = np.moveaxis(np.asarray(x, np.float32).astype(ml_dtypes.bfloat16).astype(np.float64), axis, -1)
    blocks = v.reshape(v.shape[:-1] + (-1, 32))
    amax = np.abs(blocks).max(-1, keepdims=True)
    byte = np.maximum(np.where(amax > 0, np.frexp(amax)[1] - 1 + 127, 0) - down, 1)
    scale = np.exp2(byte - 127.0)
    codes = (blocks / scale).astype(np.float32).astype(dtype).astype(np.float64)
    return np.moveaxis((codes * scale).reshape(v.shape), -1, axis)


WIDE = False


def mx_kscale(k, group=512):
    if not WIDE:
        return np.ones(k)
    levels = np.array([10, -10, 5, -5, 0])
    if group != 512:
        return np.exp2(np.random.permutation(np.resize(levels, k // group))).repeat(group)
    if k % 512:
        return np.exp2(np.random.permutation(np.resize(levels, k // 32))).repeat(32)
    a = np.empty((k // 512, 16))
    for p in range(k // 512):
        a[p, :8] = np.random.permutation(np.resize(levels, 8))
        for g in range(8):
            far = levels[np.abs(levels - a[p, g]) >= 10]
            a[p, g + 8] = far[np.random.randint(len(far))]
    return np.exp2(a.ravel()).repeat(32)


def f64(x):
    return np.asarray(x).astype(np.float64)


E2M1 = np.array([0.0, 0.5, 1.0, 1.5, 2.0, 3.0, 4.0, 6.0, -0.0, -0.5, -1.0, -1.5, -2.0, -3.0, -4.0, -6.0])


def pack_group(w):
    k, n = w.shape
    w = f64(np.asarray(w, np.float32).astype(ml_dtypes.bfloat16)).reshape(k // 32, 32, n)
    amax = np.abs(w).max(1)
    mant, ex = np.frexp(amax / 6.0)
    byte = np.clip(np.where(amax > 0, np.where(mant > 0.5, ex, ex - 1) + 127, 1), 1, 254)
    scaled = (w * np.exp2(127.0 - byte)[:, None, :]).reshape(k, n).astype(np.float32)
    c = np.ascontiguousarray(scaled.reshape(k // 4, 4, n).transpose(0, 2, 1)).astype(ml_dtypes.float4_e2m1fn).view(np.uint8) & 0xF
    return np.ascontiguousarray((c[..., 0::2] | (c[..., 1::2] << 4)).reshape(k // 4, 2 * n)), byte.astype(np.uint8)


def unpack_group(words, scales):
    p, n = words.shape[0], scales.shape[1]
    words = np.ascontiguousarray(words).reshape(p, n, 2)
    nib = np.empty((p, n, 4), np.uint8)
    nib[..., 0::2] = words & 0xF
    nib[..., 1::2] = words >> 4
    return E2M1[nib].transpose(0, 2, 1).reshape(4 * p, n) * np.repeat(np.exp2(scales.astype(np.float64) - 127.0), 32, axis=0)


G, D, M, N = 2, 256, 256, 512


def setup_inputs():
    n = np.random.standard_normal
    s = mx_kscale(D, 0)[:, None]
    w_ = [pack_group(w) for w in n((G, D, M)) / np.sqrt(D) / s]
    u_ = [pack_group(w) for w in n((G, D, M)) / np.sqrt(D) / s]
    return {
        "x": (n((G, D, N)) * s).astype(np.float32),
        "w_words": np.stack([w[0] for w in w_]),
        "w_scales": np.stack([w[1] for w in w_]),
        "u_words": np.stack([w[0] for w in u_]),
        "u_scales": np.stack([w[1] for w in u_]),
        "b": (0.5 * n((G, M, 1))).astype(np.float32),
    }


def reference(x, w_words, w_scales, u_words, u_scales, b):
    xq = mxq(f64(x), 1, "e4m3")
    h = np.stack([unpack_group(w_words[g], w_scales[g]) for g in range(G)]).transpose(0, 2, 1) @ xq
    g = np.stack([unpack_group(u_words[g], u_scales[g]) for g in range(G)]).transpose(0, 2, 1) @ xq
    h = h + f64(b)
    y = np.tanh(h) * g
    return y

@@ -1,0 +1,113 @@
+from contextlib import ExitStack
+
+import concourse.mybir as mybir
+
+G, D, M, N = 2, 256, 256, 512
+FLOPS = 2 * 2 * G * D * M * N
+
+F32 = mybir.dt.float32
+BF16 = mybir.dt.bfloat16
+I32 = mybir.dt.int32
+U32 = mybir.dt.uint32
+U8 = mybir.dt.uint8
+FP8X4 = mybir.dt.float8_e4m3fn_x4
+FP4X4 = mybir.dt.float4_e2m1fn_x4
+ACT = mybir.ActivationFunctionType
+ALU = mybir.AluOpType
+
+P = 128
+PACK = 4
+ROWS = D // PACK
+HALF = 128
+HALVES = M // HALF
+CHUNKS = ((0, 256, 160), (256, 128, 80), (384, 128, 80))
+
+
+def tile_rows_gglu_tanh_bias_kernel(tc, x, w_words, w_scales, u_words, u_scales, b, out):
+    nc = tc.nc
+    x_rows = x.rearrange("g (p j) n -> (g p) j n", j=PACK)
+
+    with ExitStack() as ctx:
+        keep = ctx.enter_context(tc.tile_pool(name="keep", bufs=1))
+        psum = ctx.enter_context(tc.psum_pool(name="psum", bufs=1))
+        ctx.enter_context(tc.manual_schedule())
+
+        words = [keep.tile([P, 2 * M], U8, align_bytes=64, name=f"words{k}") for k in range(2)]
+        planes = [keep.tile([P, M], U8, align_bytes=64, name=f"plane{k}") for k in range(2)]
+        bias = keep.tile([P, G * HALVES, 8], F32)
+        raw = [keep.tile([P, PACK, width], F32, name=f"raw{c}") for c, (start, width, cut) in enumerate(CHUNKS)]
+        grouped = [keep.tile([P, width, PACK], BF16, align_bytes=64, name=f"grouped{c}") for c, (start, width, cut) in enumerate(CHUNKS)]
+        codes = keep.tile([P, N], U32, align_bytes=64)
+        scales = keep.tile([P, N], U8, align_bytes=64)
+        warm = keep.tile([P, 8], F32)
+        warm_out = keep.tile([P, 8], F32)
+
+        def load_x(c):
+            start, width, cut = CHUNKS[c]
+            nc.sync.dma_start(out=raw[c][:], in_=x_rows[:, :, start : start + width])
+
+        def load_words(k, source):
+            nc.sync.dma_start(out=words[k][:].bitcast(I32), in_=source.rearrange("g p c -> (g p) c").bitcast(I32))
+
+        def load_plane(k, source):
+            rows = source.rearrange("g f m -> (g f) m").bitcast(I32)
+            for q in range(4):
+                nc.sync.dma_start(out=planes[k][32 * q : 32 * q + 4, :].bitcast(I32), in_=rows[4 * q : 4 * q + 4, :])
+
+        nc.vector.memset(planes[0][:].bitcast(I32), 0)
+        nc.vector.memset(warm[:], 0.0)
+        nc.vector.memset(planes[1][:].bitcast(I32), 0)
+        nc.scalar.activation(out=warm_out[:], in_=warm[:], func=ACT.Tanh)
+
+        load_x(0)
+        load_plane(0, w_scales)
+        load_words(0, w_words)
+        load_x(1)
+        load_x(2)
+        with nc.allow_non_contiguous_dma(reason="one bias value to a partition"):
+            nc.sync.dma_start(out=bias[:, :, 0:1], in_=b.rearrange("g (h p) o -> p (g h) o", p=HALF))
+        load_plane(1, u_scales)
+        load_words(1, u_words)
+
+        def interleave(engine_copy, c, lo, hi):
+            engine_copy(
+                out=grouped[c][:, lo:hi, :].rearrange("p (a i) j -> p a j i", i=4),
+                in_=raw[c][:, :, lo:hi].rearrange("p j (a i) -> p a j i", i=4),
+            )
+
+        for c, (start, width, cut) in enumerate(CHUNKS):
+            interleave(nc.scalar.copy, c, cut, width)
+            interleave(nc.vector.tensor_copy, c, 0, cut)
+            nc.vector.quantize_mx(
+                out=codes[:, start : start + width].bitcast(FP8X4),
+                scales=scales[:, start : start + width],
+                in_=grouped[c][:].rearrange("p n j -> p (n j)"),
+            )
+
+        banks = {}
+        for h in range(HALVES):
+            for k in range(2):
+                for g in range(G):
+                    rows = slice(ROWS * g, ROWS * (g + 1))
+                    bank = psum.tile([HALF, N], F32, name=f"bank{h}{k}{g}")
+                    banks[h, k, g] = bank
+                    nc.tensor.matmul_mx(
+                        out=bank[:],
+                        lhsT=words[k][rows, 2 * HALF * h : 2 * HALF * (h + 1)].bitcast(FP4X4),
+                        lhsT_scale=planes[k][rows, HALF * h : HALF * (h + 1)],
+                        rhs=codes[rows, :].bitcast(FP8X4),
+                        rhs_scale=scales[rows, :],
+                        start=True,
+                        stop=True,
+                    )
+
+        for h in range(HALVES):
+            for g in range(G):
+                gate = keep.tile([P, N], F32, name=f"gate{h}{g}")
+                result = keep.tile([P, N], F32, name=f"result{h}{g}")
+                unit = g * HALVES + h
+                nc.scalar.activation(out=gate[:], in_=banks[h, 0, g][:], func=ACT.Tanh, bias=bias[:, unit, 0:1])
+                last = h == HALVES - 1 and g == G - 1
+                for lo, hi in ((0, 256), (256, 512)) if last else ((0, N),):
+                    nc.vector.tensor_tensor(out=result[:, lo:hi], in0=banks[h, 1, g][:, lo:hi], in1=gate[:, lo:hi], op=ALU.mult)
+                    nc.sync.dma_start(out=out[g, HALF * h : HALF * (h + 1), lo:hi], in_=result[:, lo:hi])

@@ -17,10 +17,11 @@ ALU = mybir.AluOpType
 
 P = 128
 PACK = 4
+PAIR = 2
 ROWS = D // PACK
 HALF = 128
 HALVES = M // HALF
-CHUNKS = ((0, 256, 160), (256, 128, 80), (384, 128, 80))
+WIDTH = N // 2
 
 
 def tile_rows_gglu_tanh_bias_kernel(tc, x, w_words, w_scales, u_words, u_scales, b, out):
@@ -35,16 +36,13 @@ def tile_rows_gglu_tanh_bias_kernel(tc, x, w_words, w_scales, u_words, u_scales,
         words = [keep.tile([P, 2 * M], U8, align_bytes=64, name=f"words{k}") for k in range(2)]
         planes = [keep.tile([P, M], U8, align_bytes=64, name=f"plane{k}") for k in range(2)]
         bias = keep.tile([P, G * HALVES, 8], F32)
-        raw = [keep.tile([P, PACK, width], F32, name=f"raw{c}") for c, (start, width, cut) in enumerate(CHUNKS)]
-        grouped = [keep.tile([P, width, PACK], BF16, align_bytes=64, name=f"grouped{c}") for c, (start, width, cut) in enumerate(CHUNKS)]
+        front = keep.tile([P, PAIR, N], F32)
+        back = [keep.tile([P, PAIR, WIDTH], F32, name=f"back{c}") for c in range(2)]
+        grouped = keep.tile([P, N, PACK], BF16, align_bytes=64)
         codes = keep.tile([P, N], U32, align_bytes=64)
         scales = keep.tile([P, N], U8, align_bytes=64)
         warm = keep.tile([P, 8], F32)
         warm_out = keep.tile([P, 8], F32)
-
-        def load_x(c):
-            start, width, cut = CHUNKS[c]
-            nc.sync.dma_start(out=raw[c][:], in_=x_rows[:, :, start : start + width])
 
         def load_words(k, source):
             nc.sync.dma_start(out=words[k][:].bitcast(I32), in_=source.rearrange("g p c -> (g p) c").bitcast(I32))
@@ -54,35 +52,43 @@ def tile_rows_gglu_tanh_bias_kernel(tc, x, w_words, w_scales, u_words, u_scales,
             for q in range(4):
                 nc.sync.dma_start(out=planes[k][32 * q : 32 * q + 4, :].bitcast(I32), in_=rows[4 * q : 4 * q + 4, :])
 
+        def interleave(engine_copy, source, first, place, lo, hi):
+            engine_copy(
+                out=grouped[:, lo:hi, place : place + PAIR],
+                in_=source[:, :, lo - first : hi - first].rearrange("p j n -> p n j"),
+            )
+
+        def quantize(lo, hi):
+            nc.vector.quantize_mx(
+                out=codes[:, lo:hi].bitcast(FP8X4),
+                scales=scales[:, lo:hi],
+                in_=grouped[:, lo:hi, :].rearrange("p n j -> p (n j)"),
+            )
+
         nc.vector.memset(planes[0][:].bitcast(I32), 0)
         nc.vector.memset(warm[:], 0.0)
         nc.vector.memset(planes[1][:].bitcast(I32), 0)
         nc.scalar.activation(out=warm_out[:], in_=warm[:], func=ACT.Tanh)
 
-        load_x(0)
+        nc.sync.dma_start(out=front[:], in_=x_rows[:, :PAIR, :])
         load_plane(0, w_scales)
+        for c in range(2):
+            nc.sync.dma_start(out=back[c][:], in_=x_rows[:, PAIR:, WIDTH * c : WIDTH * (c + 1)])
         load_words(0, w_words)
-        load_x(1)
-        load_x(2)
         with nc.allow_non_contiguous_dma(reason="one bias value to a partition"):
             nc.sync.dma_start(out=bias[:, :, 0:1], in_=b.rearrange("g (h p) o -> p (g h) o", p=HALF))
         load_plane(1, u_scales)
         load_words(1, u_words)
 
-        def interleave(engine_copy, c, lo, hi):
-            engine_copy(
-                out=grouped[c][:, lo:hi, :].rearrange("p (a i) j -> p a j i", i=4),
-                in_=raw[c][:, :, lo:hi].rearrange("p j (a i) -> p a j i", i=4),
-            )
-
-        for c, (start, width, cut) in enumerate(CHUNKS):
-            interleave(nc.scalar.copy, c, cut, width)
-            interleave(nc.vector.tensor_copy, c, 0, cut)
-            nc.vector.quantize_mx(
-                out=codes[:, start : start + width].bitcast(FP8X4),
-                scales=scales[:, start : start + width],
-                in_=grouped[c][:].rearrange("p n j -> p (n j)"),
-            )
+        interleave(nc.scalar.copy, front, 0, 0, 352, 512)
+        interleave(nc.vector.tensor_copy, front, 0, 0, 0, 352)
+        interleave(nc.scalar.copy, back[0], 0, PAIR, 176, 256)
+        interleave(nc.vector.tensor_copy, back[0], 0, PAIR, 0, 176)
+        quantize(0, 256)
+        interleave(nc.scalar.copy, back[1], WIDTH, PAIR, 256, 384)
+        interleave(nc.vector.tensor_copy, back[1], WIDTH, PAIR, 384, 512)
+        quantize(256, 384)
+        quantize(384, 512)
 
         banks = {}
         for h in range(HALVES):
@@ -105,9 +111,13 @@ def tile_rows_gglu_tanh_bias_kernel(tc, x, w_words, w_scales, u_words, u_scales,
             for g in range(G):
                 gate = keep.tile([P, N], F32, name=f"gate{h}{g}")
                 result = keep.tile([P, N], F32, name=f"result{h}{g}")
-                unit = g * HALVES + h
-                nc.scalar.activation(out=gate[:], in_=banks[h, 0, g][:], func=ACT.Tanh, bias=bias[:, unit, 0:1])
-                last = h == HALVES - 1 and g == G - 1
-                for lo, hi in ((0, 256), (256, 512)) if last else ((0, N),):
-                    nc.vector.tensor_tensor(out=result[:, lo:hi], in0=banks[h, 1, g][:, lo:hi], in1=gate[:, lo:hi], op=ALU.mult)
-                    nc.sync.dma_start(out=out[g, HALF * h : HALF * (h + 1), lo:hi], in_=result[:, lo:hi])
+                rows = out[g, HALF * h : HALF * (h + 1), :]
+                first = h == 0 and g == 0
+                for c in range(2):
+                    cols = slice(WIDTH * c, WIDTH * (c + 1))
+                    nc.scalar.activation(out=gate[:, cols], in_=banks[h, 0, g][:, cols], func=ACT.Tanh, bias=bias[:, g * HALVES + h, 0:1])
+                    nc.vector.tensor_tensor(out=result[:, cols], in0=banks[h, 1, g][:, cols], in1=gate[:, cols], op=ALU.mult)
+                    if first:
+                        nc.sync.dma_start(out=rows[:, cols], in_=result[:, cols])
+                if not first:
+                    nc.sync.dma_start(out=rows, in_=result[:])

@@ -35,7 +35,8 @@ def tile_rows_gglu_tanh_bias_kernel(tc, x, w_words, w_scales, u_words, u_scales,
 
         words = [keep.tile([P, 2 * M], U8, align_bytes=64, name=f"words{k}") for k in range(2)]
         planes = [keep.tile([P, M], U8, align_bytes=64, name=f"plane{k}") for k in range(2)]
-        bias = keep.tile([P, G * HALVES, 8], F32)
+        bias_rows = keep.tile([P, G * HALVES, 32], F32, align_bytes=64)
+        bias = keep.tile([P, G * HALVES, 32], F32, align_bytes=64)
         front = keep.tile([P, PAIR, N], F32)
         back = [keep.tile([P, PAIR, WIDTH], F32, name=f"back{c}") for c in range(2)]
         grouped = keep.tile([P, N, PACK], BF16, align_bytes=64)
@@ -68,6 +69,7 @@ def tile_rows_gglu_tanh_bias_kernel(tc, x, w_words, w_scales, u_words, u_scales,
         nc.vector.memset(planes[0][:].bitcast(I32), 0)
         nc.vector.memset(warm[:], 0.0)
         nc.vector.memset(planes[1][:].bitcast(I32), 0)
+        nc.vector.memset(bias_rows[:], 0.0)
         nc.scalar.activation(out=warm_out[:], in_=warm[:], func=ACT.Tanh)
 
         nc.sync.dma_start(out=front[:], in_=x_rows[:, :PAIR, :])
@@ -75,20 +77,22 @@ def tile_rows_gglu_tanh_bias_kernel(tc, x, w_words, w_scales, u_words, u_scales,
         for c in range(2):
             nc.sync.dma_start(out=back[c][:], in_=x_rows[:, PAIR:, WIDTH * c : WIDTH * (c + 1)])
         load_words(0, w_words)
-        with nc.allow_non_contiguous_dma(reason="one bias value to a partition"):
-            nc.sync.dma_start(out=bias[:, :, 0:1], in_=b.rearrange("g (h p) o -> p (g h) o", p=HALF))
-        load_plane(1, u_scales)
         load_words(1, u_words)
+        nc.sync.dma_start(out=bias_rows[0:P:32, :, :], in_=b.rearrange("g (h q j) o -> q (g h) (j o)", q=4, j=32))
+        load_plane(1, u_scales)
 
-        interleave(nc.scalar.copy, front, 0, 0, 352, 512)
-        interleave(nc.vector.tensor_copy, front, 0, 0, 0, 352)
-        interleave(nc.scalar.copy, back[0], 0, PAIR, 176, 256)
-        interleave(nc.vector.tensor_copy, back[0], 0, PAIR, 0, 176)
-        quantize(0, 256)
-        interleave(nc.scalar.copy, back[1], WIDTH, PAIR, 256, 384)
-        interleave(nc.vector.tensor_copy, back[1], WIDTH, PAIR, 384, 512)
+        interleave(nc.scalar.copy, front, 0, 0, 336, 512)
+        interleave(nc.vector.tensor_copy, front, 0, 0, 0, 336)
+        interleave(nc.scalar.copy, back[0], 0, PAIR, 128, 256)
+        interleave(nc.vector.tensor_copy, back[0], 0, PAIR, 0, 128)
+        quantize(0, 128)
+        interleave(nc.scalar.copy, back[1], WIDTH, PAIR, 384, 512)
+        interleave(nc.vector.tensor_copy, back[1], WIDTH, PAIR, 256, 384)
+        quantize(128, 256)
         quantize(256, 384)
         quantize(384, 512)
+
+        nc.vector.transpose(out=bias[:].rearrange("p c j -> p (c j)"), in_=bias_rows[:].rearrange("p c j -> p (c j)"))
 
         banks = {}
         for h in range(HALVES):

@@ -42,8 +42,6 @@ def tile_rows_gglu_tanh_bias_kernel(tc, x, w_words, w_scales, u_words, u_scales,
         grouped = keep.tile([P, N, PACK], BF16, align_bytes=64)
         codes = keep.tile([P, N], U32, align_bytes=64)
         scales = keep.tile([P, N], U8, align_bytes=64)
-        warm = keep.tile([P, 8], F32)
-        warm_out = keep.tile([P, 8], F32)
 
         def load_words(k, source):
             nc.sync.dma_start(out=words[k][:].bitcast(I32), in_=source.rearrange("g p c -> (g p) c").bitcast(I32))
@@ -67,10 +65,8 @@ def tile_rows_gglu_tanh_bias_kernel(tc, x, w_words, w_scales, u_words, u_scales,
             )
 
         nc.vector.memset(planes[0][:].bitcast(I32), 0)
-        nc.vector.memset(warm[:], 0.0)
         nc.vector.memset(planes[1][:].bitcast(I32), 0)
         nc.vector.memset(bias_rows[:], 0.0)
-        nc.scalar.activation(out=warm_out[:], in_=warm[:], func=ACT.Tanh)
 
         nc.sync.dma_start(out=front[:], in_=x_rows[:, :PAIR, :])
         load_plane(0, w_scales)

@@ -22,6 +22,7 @@ ROWS = D // PACK
 HALF = 128
 HALVES = M // HALF
 WIDTH = N // 2
+RUN = 4
 
 
 def tile_rows_gglu_tanh_bias_kernel(tc, x, w_words, w_scales, u_words, u_scales, b, out):
@@ -35,13 +36,16 @@ def tile_rows_gglu_tanh_bias_kernel(tc, x, w_words, w_scales, u_words, u_scales,
 
         words = [keep.tile([P, 2 * M], U8, align_bytes=64, name=f"words{k}") for k in range(2)]
         planes = [keep.tile([P, M], U8, align_bytes=64, name=f"plane{k}") for k in range(2)]
-        bias_rows = keep.tile([P, G * HALVES, 32], F32, align_bytes=64)
-        bias = keep.tile([P, G * HALVES, 32], F32, align_bytes=64)
-        front = keep.tile([P, PAIR, N], F32)
-        back = [keep.tile([P, PAIR, WIDTH], F32, name=f"back{c}") for c in range(2)]
+        bias = keep.tile([P, G * HALVES, 1], F32)
+        raw = [keep.tile([P, PACK, WIDTH], F32, name=f"raw{c}") for c in range(2)]
         grouped = keep.tile([P, N, PACK], BF16, align_bytes=64)
-        codes = keep.tile([P, N], U32, align_bytes=64)
-        scales = keep.tile([P, N], U8, align_bytes=64)
+        codes = keep.tile([P, WIDTH + N], U32, align_bytes=64)
+        scales = keep.tile([P, WIDTH + N], U8, align_bytes=64)
+        banks = {}
+        for h in range(HALVES):
+            for k in range(2):
+                for g in range(G):
+                    banks[h, k, g] = psum.tile([HALF, N], F32, name=f"bank{h}{k}{g}")
 
         def load_words(k, source):
             nc.sync.dma_start(out=words[k][:].bitcast(I32), in_=source.rearrange("g p c -> (g p) c").bitcast(I32))
@@ -51,73 +55,74 @@ def tile_rows_gglu_tanh_bias_kernel(tc, x, w_words, w_scales, u_words, u_scales,
             for q in range(4):
                 nc.sync.dma_start(out=planes[k][32 * q : 32 * q + 4, :].bitcast(I32), in_=rows[4 * q : 4 * q + 4, :])
 
-        def interleave(engine_copy, source, first, place, lo, hi):
+        def interleave(engine_copy, lo, hi):
+            c = lo // WIDTH
             engine_copy(
-                out=grouped[:, lo:hi, place : place + PAIR],
-                in_=source[:, :, lo - first : hi - first].rearrange("p j n -> p n j"),
+                out=grouped[:, lo:hi, :].rearrange("p (c i) j -> p c j i", i=RUN),
+                in_=raw[c][:, :, lo - WIDTH * c : hi - WIDTH * c].rearrange("p j (c i) -> p c j i", i=RUN),
             )
 
         def quantize(lo, hi):
             nc.vector.quantize_mx(
-                out=codes[:, lo:hi].bitcast(FP8X4),
-                scales=scales[:, lo:hi],
+                out=codes[:, WIDTH + lo : WIDTH + hi].bitcast(FP8X4),
+                scales=scales[:, WIDTH + lo : WIDTH + hi],
                 in_=grouped[:, lo:hi, :].rearrange("p n j -> p (n j)"),
             )
 
-        nc.vector.memset(planes[0][:].bitcast(I32), 0)
-        nc.vector.memset(planes[1][:].bitcast(I32), 0)
-        nc.vector.memset(bias_rows[:], 0.0)
-
-        nc.sync.dma_start(out=front[:], in_=x_rows[:, :PAIR, :])
-        load_plane(0, w_scales)
-        for c in range(2):
-            nc.sync.dma_start(out=back[c][:], in_=x_rows[:, PAIR:, WIDTH * c : WIDTH * (c + 1)])
-        load_words(0, w_words)
-        load_words(1, u_words)
-        nc.sync.dma_start(out=bias_rows[0:P:32, :, :], in_=b.rearrange("g (h q j) o -> q (g h) (j o)", q=4, j=32))
-        load_plane(1, u_scales)
-
-        interleave(nc.scalar.copy, front, 0, 0, 336, 512)
-        interleave(nc.vector.tensor_copy, front, 0, 0, 0, 336)
-        interleave(nc.scalar.copy, back[0], 0, PAIR, 128, 256)
-        interleave(nc.vector.tensor_copy, back[0], 0, PAIR, 0, 128)
-        quantize(0, 128)
-        interleave(nc.scalar.copy, back[1], WIDTH, PAIR, 384, 512)
-        interleave(nc.vector.tensor_copy, back[1], WIDTH, PAIR, 256, 384)
-        quantize(128, 256)
-        quantize(256, 384)
-        quantize(384, 512)
-
-        nc.vector.transpose(out=bias[:].rearrange("p c j -> p (c j)"), in_=bias_rows[:].rearrange("p c j -> p (c j)"))
-
-        banks = {}
-        for h in range(HALVES):
+        def multiply(h, first):
             for k in range(2):
                 for g in range(G):
                     rows = slice(ROWS * g, ROWS * (g + 1))
-                    bank = psum.tile([HALF, N], F32, name=f"bank{h}{k}{g}")
-                    banks[h, k, g] = bank
                     nc.tensor.matmul_mx(
-                        out=bank[:],
+                        out=banks[h, k, g][:],
                         lhsT=words[k][rows, 2 * HALF * h : 2 * HALF * (h + 1)].bitcast(FP4X4),
                         lhsT_scale=planes[k][rows, HALF * h : HALF * (h + 1)],
-                        rhs=codes[rows, :].bitcast(FP8X4),
-                        rhs_scale=scales[rows, :],
+                        rhs=codes[rows, first : first + N].bitcast(FP8X4),
+                        rhs_scale=scales[rows, first : first + N],
                         start=True,
                         stop=True,
                     )
 
-        for h in range(HALVES):
-            for g in range(G):
-                gate = keep.tile([P, N], F32, name=f"gate{h}{g}")
-                result = keep.tile([P, N], F32, name=f"result{h}{g}")
-                rows = out[g, HALF * h : HALF * (h + 1), :]
-                first = h == 0 and g == 0
-                for c in range(2):
-                    cols = slice(WIDTH * c, WIDTH * (c + 1))
-                    nc.scalar.activation(out=gate[:, cols], in_=banks[h, 0, g][:, cols], func=ACT.Tanh, bias=bias[:, g * HALVES + h, 0:1])
-                    nc.vector.tensor_tensor(out=result[:, cols], in0=banks[h, 1, g][:, cols], in1=gate[:, cols], op=ALU.mult)
-                    if first:
-                        nc.sync.dma_start(out=rows[:, cols], in_=result[:, cols])
-                if not first:
-                    nc.sync.dma_start(out=rows, in_=result[:])
+        def gate_and_store(h, g, bank_halves, c0):
+            width = WIDTH * len(bank_halves)
+            gate = keep.tile([P, width], F32, name=f"gate{h}{g}{c0}")
+            result = keep.tile([P, width], F32, name=f"result{h}{g}{c0}")
+            for i, c in enumerate(bank_halves):
+                cols = slice(WIDTH * c, WIDTH * (c + 1))
+                mine = slice(WIDTH * i, WIDTH * (i + 1))
+                nc.scalar.activation(out=gate[:, mine], in_=banks[h, 0, g][:, cols], func=ACT.Tanh, bias=bias[:, g * HALVES + h, 0:1])
+                nc.vector.tensor_tensor(out=result[:, mine], in0=banks[h, 1, g][:, cols], in1=gate[:, mine], op=ALU.mult)
+            nc.sync.dma_start(out=out[g, HALF * h : HALF * (h + 1), c0 : c0 + width], in_=result[:])
+
+        nc.vector.memset(planes[0][:].bitcast(I32), 0)
+        nc.vector.memset(planes[1][:].bitcast(I32), 0)
+        nc.vector.memset(codes[:, :WIDTH], 0)
+        nc.vector.memset(scales[:, :WIDTH].bitcast(I32), 0)
+
+        load_words(0, w_words)
+        nc.sync.dma_start(out=raw[0][:], in_=x_rows[:, :, :WIDTH])
+        load_plane(0, w_scales)
+        nc.sync.dma_start(out=raw[1][:], in_=x_rows[:, :, WIDTH:])
+        load_words(1, u_words)
+        load_plane(1, u_scales)
+        with nc.allow_non_contiguous_dma(reason="one bias value a partition"):
+            nc.sync.dma_start(out=bias[:], in_=b.rearrange("g (h p) o -> p (g h) o", p=HALF))
+
+        for c in range(2):
+            lo = WIDTH * c
+            interleave(nc.scalar.copy, lo + 176, lo + 256)
+            interleave(nc.vector.tensor_copy, lo, lo + 128)
+            interleave(nc.vector.tensor_copy, lo + 128, lo + 176)
+            quantize(lo, lo + 128)
+            quantize(lo + 128, lo + 256)
+            if c == 0:
+                multiply(0, 0)
+
+        for g in range(G):
+            gate_and_store(0, g, [1], 0)
+        multiply(1, WIDTH)
+        multiply(0, WIDTH)
+        for g in range(G):
+            gate_and_store(1, g, [0, 1], 0)
+        for g in range(G):
+            gate_and_store(0, g, [1], WIDTH)

@@ -22,7 +22,6 @@ ROWS = D // PACK
 HALF = 128
 HALVES = M // HALF
 WIDTH = N // 2
-RUN = 4
 
 
 def tile_rows_gglu_tanh_bias_kernel(tc, x, w_words, w_scales, u_words, u_scales, b, out):
@@ -36,8 +35,9 @@ def tile_rows_gglu_tanh_bias_kernel(tc, x, w_words, w_scales, u_words, u_scales,
 
         words = [keep.tile([P, 2 * M], U8, align_bytes=64, name=f"words{k}") for k in range(2)]
         planes = [keep.tile([P, M], U8, align_bytes=64, name=f"plane{k}") for k in range(2)]
-        bias = keep.tile([P, G * HALVES, 1], F32)
-        raw = [keep.tile([P, PACK, WIDTH], F32, name=f"raw{c}") for c in range(2)]
+        bias_rows = keep.tile([P, G * HALVES, 32], F32, align_bytes=64)
+        bias = keep.tile([P, G * HALVES, 32], F32, align_bytes=64)
+        raw = [[keep.tile([P, PAIR, WIDTH], F32, name=f"raw{c}{r}") for r in range(2)] for c in range(2)]
         grouped = keep.tile([P, N, PACK], BF16, align_bytes=64)
         codes = keep.tile([P, WIDTH + N], U32, align_bytes=64)
         scales = keep.tile([P, WIDTH + N], U8, align_bytes=64)
@@ -46,6 +46,7 @@ def tile_rows_gglu_tanh_bias_kernel(tc, x, w_words, w_scales, u_words, u_scales,
             for k in range(2):
                 for g in range(G):
                     banks[h, k, g] = psum.tile([HALF, N], F32, name=f"bank{h}{k}{g}")
+        gates = {}
 
         def load_words(k, source):
             nc.sync.dma_start(out=words[k][:].bitcast(I32), in_=source.rearrange("g p c -> (g p) c").bitcast(I32))
@@ -55,11 +56,14 @@ def tile_rows_gglu_tanh_bias_kernel(tc, x, w_words, w_scales, u_words, u_scales,
             for q in range(4):
                 nc.sync.dma_start(out=planes[k][32 * q : 32 * q + 4, :].bitcast(I32), in_=rows[4 * q : 4 * q + 4, :])
 
-        def interleave(engine_copy, lo, hi):
+        def load_x(c, r):
+            nc.sync.dma_start(out=raw[c][r][:], in_=x_rows[:, PAIR * r : PAIR * (r + 1), WIDTH * c : WIDTH * (c + 1)])
+
+        def interleave(engine_copy, r, lo, hi):
             c = lo // WIDTH
             engine_copy(
-                out=grouped[:, lo:hi, :].rearrange("p (c i) j -> p c j i", i=RUN),
-                in_=raw[c][:, :, lo - WIDTH * c : hi - WIDTH * c].rearrange("p j (c i) -> p c j i", i=RUN),
+                out=grouped[:, lo:hi, PAIR * r : PAIR * (r + 1)],
+                in_=raw[c][r][:, :, lo - WIDTH * c : hi - WIDTH * c].rearrange("p j n -> p n j"),
             )
 
         def quantize(lo, hi):
@@ -69,60 +73,71 @@ def tile_rows_gglu_tanh_bias_kernel(tc, x, w_words, w_scales, u_words, u_scales,
                 in_=grouped[:, lo:hi, :].rearrange("p n j -> p (n j)"),
             )
 
-        def multiply(h, first):
-            for k in range(2):
-                for g in range(G):
-                    rows = slice(ROWS * g, ROWS * (g + 1))
-                    nc.tensor.matmul_mx(
-                        out=banks[h, k, g][:],
-                        lhsT=words[k][rows, 2 * HALF * h : 2 * HALF * (h + 1)].bitcast(FP4X4),
-                        lhsT_scale=planes[k][rows, HALF * h : HALF * (h + 1)],
-                        rhs=codes[rows, first : first + N].bitcast(FP8X4),
-                        rhs_scale=scales[rows, first : first + N],
-                        start=True,
-                        stop=True,
-                    )
+        def multiply(h, k, first):
+            for g in range(G):
+                rows = slice(ROWS * g, ROWS * (g + 1))
+                nc.tensor.matmul_mx(
+                    out=banks[h, k, g][:],
+                    lhsT=words[k][rows, 2 * HALF * h : 2 * HALF * (h + 1)].bitcast(FP4X4),
+                    lhsT_scale=planes[k][rows, HALF * h : HALF * (h + 1)],
+                    rhs=codes[rows, first : first + N].bitcast(FP8X4),
+                    rhs_scale=scales[rows, first : first + N],
+                    start=True,
+                    stop=True,
+                )
 
-        def gate_and_store(h, g, bank_halves, c0):
-            width = WIDTH * len(bank_halves)
-            gate = keep.tile([P, width], F32, name=f"gate{h}{g}{c0}")
-            result = keep.tile([P, width], F32, name=f"result{h}{g}{c0}")
-            for i, c in enumerate(bank_halves):
-                cols = slice(WIDTH * c, WIDTH * (c + 1))
-                mine = slice(WIDTH * i, WIDTH * (i + 1))
-                nc.scalar.activation(out=gate[:, mine], in_=banks[h, 0, g][:, cols], func=ACT.Tanh, bias=bias[:, g * HALVES + h, 0:1])
-                nc.vector.tensor_tensor(out=result[:, mine], in0=banks[h, 1, g][:, cols], in1=gate[:, mine], op=ALU.mult)
-            nc.sync.dma_start(out=out[g, HALF * h : HALF * (h + 1), c0 : c0 + width], in_=result[:])
+        def activate(h, c):
+            for g in range(G):
+                gates[h, g, c] = keep.tile([P, WIDTH], F32, name=f"gate{h}{g}{c}")
+                nc.scalar.activation(out=gates[h, g, c][:], in_=banks[h, 0, g][:, WIDTH:], func=ACT.Tanh, bias=bias[:, g * HALVES + h, 0:1])
 
+        def gate_and_store(h, c, bank_half):
+            for g in range(G):
+                result = keep.tile([P, WIDTH], F32, name=f"result{h}{g}{c}")
+                cols = slice(WIDTH * bank_half, WIDTH * (bank_half + 1))
+                nc.vector.tensor_tensor(out=result[:], in0=banks[h, 1, g][:, cols], in1=gates[h, g, c][:], op=ALU.mult)
+                nc.sync.dma_start(out=out[g, HALF * h : HALF * (h + 1), WIDTH * c : WIDTH * (c + 1)], in_=result[:])
+
+        nc.vector.memset(bias_rows[:], 0.0)
         nc.vector.memset(planes[0][:].bitcast(I32), 0)
         nc.vector.memset(planes[1][:].bitcast(I32), 0)
         nc.vector.memset(codes[:, :WIDTH], 0)
         nc.vector.memset(scales[:, :WIDTH].bitcast(I32), 0)
 
+        load_x(0, 0)
+        nc.sync.dma_start(out=bias_rows[0:P:32, :, :], in_=b.rearrange("g (h q j) o -> q (g h) (j o)", q=4, j=32))
+        load_x(0, 1)
         load_words(0, w_words)
-        nc.sync.dma_start(out=raw[0][:], in_=x_rows[:, :, :WIDTH])
         load_plane(0, w_scales)
-        nc.sync.dma_start(out=raw[1][:], in_=x_rows[:, :, WIDTH:])
+        load_x(1, 0)
+        load_x(1, 1)
         load_words(1, u_words)
         load_plane(1, u_scales)
-        with nc.allow_non_contiguous_dma(reason="one bias value a partition"):
-            nc.sync.dma_start(out=bias[:], in_=b.rearrange("g (h p) o -> p (g h) o", p=HALF))
 
         for c in range(2):
             lo = WIDTH * c
-            interleave(nc.scalar.copy, lo + 176, lo + 256)
-            interleave(nc.vector.tensor_copy, lo, lo + 128)
-            interleave(nc.vector.tensor_copy, lo + 128, lo + 176)
+            interleave(nc.scalar.copy, 0, lo + 128, lo + 256)
+            interleave(nc.vector.tensor_copy, 0, lo, lo + 128)
+            if c == 0:
+                nc.vector.transpose(out=bias[:].rearrange("p c j -> p (c j)"), in_=bias_rows[:].rearrange("p c j -> p (c j)"))
+            interleave(nc.scalar.copy, 1, lo + 176, lo + 256)
+            interleave(nc.vector.tensor_copy, 1, lo, lo + 128)
+            interleave(nc.vector.tensor_copy, 1, lo + 128, lo + 176)
             quantize(lo, lo + 128)
             quantize(lo + 128, lo + 256)
-            if c == 0:
-                multiply(0, 0)
 
-        for g in range(G):
-            gate_and_store(0, g, [1], 0)
-        multiply(1, WIDTH)
-        multiply(0, WIDTH)
-        for g in range(G):
-            gate_and_store(1, g, [0, 1], 0)
-        for g in range(G):
-            gate_and_store(0, g, [1], WIDTH)
+        multiply(0, 0, 0)
+        multiply(1, 0, 0)
+        multiply(0, 1, 0)
+        activate(0, 0)
+        activate(1, 0)
+        gate_and_store(0, 0, 1)
+        multiply(1, 1, WIDTH)
+        multiply(1, 0, WIDTH)
+        multiply(0, 0, WIDTH)
+        multiply(0, 1, WIDTH)
+        gate_and_store(1, 0, 0)
+        activate(1, 1)
+        gate_and_store(1, 1, 1)
+        activate(0, 1)
+        gate_and_store(0, 1, 1)

@@ -22,6 +22,9 @@ ROWS = D // PACK
 HALF = 128
 HALVES = M // HALF
 WIDTH = N // 2
+RUN = 4
+W, U = 0, 1
+EARLY, LATE = 0, WIDTH
 
 
 def tile_rows_gglu_tanh_bias_kernel(tc, x, w_words, w_scales, u_words, u_scales, b, out):
@@ -37,7 +40,8 @@ def tile_rows_gglu_tanh_bias_kernel(tc, x, w_words, w_scales, u_words, u_scales,
         planes = [keep.tile([P, M], U8, align_bytes=64, name=f"plane{k}") for k in range(2)]
         bias_rows = keep.tile([P, G * HALVES, 32], F32, align_bytes=64)
         bias = keep.tile([P, G * HALVES, 32], F32, align_bytes=64)
-        raw = [[keep.tile([P, PAIR, WIDTH], F32, name=f"raw{c}{r}") for r in range(2)] for c in range(2)]
+        left = [keep.tile([P, PAIR, WIDTH], F32, name=f"left{r}") for r in range(2)]
+        right = keep.tile([P, PACK, WIDTH], F32)
         grouped = keep.tile([P, N, PACK], BF16, align_bytes=64)
         codes = keep.tile([P, WIDTH + N], U32, align_bytes=64)
         scales = keep.tile([P, WIDTH + N], U8, align_bytes=64)
@@ -51,19 +55,21 @@ def tile_rows_gglu_tanh_bias_kernel(tc, x, w_words, w_scales, u_words, u_scales,
         def load_words(k, source):
             nc.sync.dma_start(out=words[k][:].bitcast(I32), in_=source.rearrange("g p c -> (g p) c").bitcast(I32))
 
-        def load_plane(k, source):
+        def load_plane(k, source, quadrants):
             rows = source.rearrange("g f m -> (g f) m").bitcast(I32)
-            for q in range(4):
+            for q in quadrants:
                 nc.sync.dma_start(out=planes[k][32 * q : 32 * q + 4, :].bitcast(I32), in_=rows[4 * q : 4 * q + 4, :])
 
-        def load_x(c, r):
-            nc.sync.dma_start(out=raw[c][r][:], in_=x_rows[:, PAIR * r : PAIR * (r + 1), WIDTH * c : WIDTH * (c + 1)])
-
-        def interleave(engine_copy, r, lo, hi):
-            c = lo // WIDTH
+        def interleave_left(engine_copy, r, lo, hi):
             engine_copy(
                 out=grouped[:, lo:hi, PAIR * r : PAIR * (r + 1)],
-                in_=raw[c][r][:, :, lo - WIDTH * c : hi - WIDTH * c].rearrange("p j n -> p n j"),
+                in_=left[r][:, :, lo:hi].rearrange("p j n -> p n j"),
+            )
+
+        def interleave_right(engine_copy, lo, hi):
+            engine_copy(
+                out=grouped[:, WIDTH + lo : WIDTH + hi, :].rearrange("p (c i) j -> p c j i", i=RUN),
+                in_=right[:, :, lo:hi].rearrange("p j (c i) -> p c j i", i=RUN),
             )
 
         def quantize(lo, hi):
@@ -73,71 +79,86 @@ def tile_rows_gglu_tanh_bias_kernel(tc, x, w_words, w_scales, u_words, u_scales,
                 in_=grouped[:, lo:hi, :].rearrange("p n j -> p (n j)"),
             )
 
-        def multiply(h, k, first):
-            for g in range(G):
-                rows = slice(ROWS * g, ROWS * (g + 1))
-                nc.tensor.matmul_mx(
-                    out=banks[h, k, g][:],
-                    lhsT=words[k][rows, 2 * HALF * h : 2 * HALF * (h + 1)].bitcast(FP4X4),
-                    lhsT_scale=planes[k][rows, HALF * h : HALF * (h + 1)],
-                    rhs=codes[rows, first : first + N].bitcast(FP8X4),
-                    rhs_scale=scales[rows, first : first + N],
-                    start=True,
-                    stop=True,
-                )
+        def multiply(g, k, h, first):
+            rows = slice(ROWS * g, ROWS * (g + 1))
+            nc.tensor.matmul_mx(
+                out=banks[h, k, g][:],
+                lhsT=words[k][rows, 2 * HALF * h : 2 * HALF * (h + 1)].bitcast(FP4X4),
+                lhsT_scale=planes[k][rows, HALF * h : HALF * (h + 1)],
+                rhs=codes[rows, first : first + N].bitcast(FP8X4),
+                rhs_scale=scales[rows, first : first + N],
+                start=True,
+                stop=True,
+            )
 
-        def activate(h, c):
-            for g in range(G):
-                gates[h, g, c] = keep.tile([P, WIDTH], F32, name=f"gate{h}{g}{c}")
-                nc.scalar.activation(out=gates[h, g, c][:], in_=banks[h, 0, g][:, WIDTH:], func=ACT.Tanh, bias=bias[:, g * HALVES + h, 0:1])
+        def bank_columns(c, first):
+            return slice(WIDTH * (c + 1) - first, WIDTH * (c + 2) - first)
 
-        def gate_and_store(h, c, bank_half):
-            for g in range(G):
-                result = keep.tile([P, WIDTH], F32, name=f"result{h}{g}{c}")
-                cols = slice(WIDTH * bank_half, WIDTH * (bank_half + 1))
-                nc.vector.tensor_tensor(out=result[:], in0=banks[h, 1, g][:, cols], in1=gates[h, g, c][:], op=ALU.mult)
-                nc.sync.dma_start(out=out[g, HALF * h : HALF * (h + 1), WIDTH * c : WIDTH * (c + 1)], in_=result[:])
+        def activate(g, h, c, first):
+            gates[g, h, c] = keep.tile([P, WIDTH], F32, name=f"gate{g}{h}{c}")
+            nc.scalar.activation(out=gates[g, h, c][:], in_=banks[h, W, g][:, bank_columns(c, first)], func=ACT.Tanh, bias=bias[:, g * HALVES + h, 0:1])
 
+        def gate_and_store(g, h, c, first):
+            result = keep.tile([P, WIDTH], F32, name=f"result{g}{h}{c}")
+            nc.vector.tensor_tensor(out=result[:], in0=banks[h, U, g][:, bank_columns(c, first)], in1=gates[g, h, c][:], op=ALU.mult)
+            nc.sync.dma_start(out=out[g, HALF * h : HALF * (h + 1), WIDTH * c : WIDTH * (c + 1)], in_=result[:])
+
+        nc.vector.memset(planes[W][:].bitcast(I32), 0)
+        nc.vector.memset(planes[U][:].bitcast(I32), 0)
         nc.vector.memset(bias_rows[:], 0.0)
-        nc.vector.memset(planes[0][:].bitcast(I32), 0)
-        nc.vector.memset(planes[1][:].bitcast(I32), 0)
         nc.vector.memset(codes[:, :WIDTH], 0)
         nc.vector.memset(scales[:, :WIDTH].bitcast(I32), 0)
 
-        load_x(0, 0)
+        for r in range(2):
+            nc.sync.dma_start(out=left[r][:], in_=x_rows[:, PAIR * r : PAIR * (r + 1), :WIDTH])
+        load_words(W, w_words)
+        load_plane(W, w_scales, (0, 1, 2, 3))
+        nc.sync.dma_start(out=right[:], in_=x_rows[:, :, WIDTH:])
         nc.sync.dma_start(out=bias_rows[0:P:32, :, :], in_=b.rearrange("g (h q j) o -> q (g h) (j o)", q=4, j=32))
-        load_x(0, 1)
-        load_words(0, w_words)
-        load_plane(0, w_scales)
-        load_x(1, 0)
-        load_x(1, 1)
-        load_words(1, u_words)
-        load_plane(1, u_scales)
+        load_words(U, u_words)
+        load_plane(U, u_scales, (2, 3, 0, 1))
 
-        for c in range(2):
-            lo = WIDTH * c
-            interleave(nc.scalar.copy, 0, lo + 128, lo + 256)
-            interleave(nc.vector.tensor_copy, 0, lo, lo + 128)
-            if c == 0:
-                nc.vector.transpose(out=bias[:].rearrange("p c j -> p (c j)"), in_=bias_rows[:].rearrange("p c j -> p (c j)"))
-            interleave(nc.scalar.copy, 1, lo + 176, lo + 256)
-            interleave(nc.vector.tensor_copy, 1, lo, lo + 128)
-            interleave(nc.vector.tensor_copy, 1, lo + 128, lo + 176)
-            quantize(lo, lo + 128)
-            quantize(lo + 128, lo + 256)
+        interleave_left(nc.scalar.copy, 0, 128, 256)
+        interleave_left(nc.vector.tensor_copy, 0, 0, 128)
+        interleave_left(nc.scalar.copy, 1, 176, 256)
+        interleave_left(nc.vector.tensor_copy, 1, 0, 128)
+        interleave_left(nc.vector.tensor_copy, 1, 128, 176)
+        quantize(0, 128)
+        quantize(128, 256)
 
-        multiply(0, 0, 0)
-        multiply(1, 0, 0)
-        multiply(0, 1, 0)
-        activate(0, 0)
-        activate(1, 0)
-        gate_and_store(0, 0, 1)
-        multiply(1, 1, WIDTH)
-        multiply(1, 0, WIDTH)
-        multiply(0, 0, WIDTH)
-        multiply(0, 1, WIDTH)
-        gate_and_store(1, 0, 0)
-        activate(1, 1)
-        gate_and_store(1, 1, 1)
-        activate(0, 1)
-        gate_and_store(0, 1, 1)
+        interleave_right(nc.scalar.copy, 176, 256)
+        interleave_right(nc.vector.tensor_copy, 0, 128)
+        interleave_right(nc.vector.tensor_copy, 128, 176)
+        nc.vector.transpose(out=bias[:].rearrange("p c j -> p (c j)"), in_=bias_rows[:].rearrange("p c j -> p (c j)"))
+        quantize(256, 384)
+        quantize(384, 512)
+
+        multiply(0, W, 0, EARLY)
+        multiply(1, W, 0, EARLY)
+        multiply(0, W, 1, EARLY)
+        multiply(1, U, 0, EARLY)
+        multiply(0, U, 0, EARLY)
+        activate(1, 0, 0, EARLY)
+        activate(0, 0, 0, EARLY)
+        activate(0, 1, 0, EARLY)
+        gate_and_store(1, 0, 0, EARLY)
+        gate_and_store(0, 0, 0, EARLY)
+
+        multiply(1, W, 1, LATE)
+        multiply(0, U, 1, LATE)
+        multiply(1, U, 1, LATE)
+        multiply(0, W, 1, LATE)
+        activate(1, 1, 0, LATE)
+        activate(1, 1, 1, LATE)
+        activate(0, 1, 1, LATE)
+        gate_and_store(0, 1, 0, LATE)
+        gate_and_store(1, 1, 0, LATE)
+        gate_and_store(1, 1, 1, LATE)
+        gate_and_store(0, 1, 1, LATE)
+
+        for k in (W, U):
+            for g in (1, 0):
+                multiply(g, k, 0, LATE)
+        for g in (1, 0):
+            activate(g, 0, 1, LATE)
+            gate_and_store(g, 0, 1, LATE)

@@ -17,14 +17,12 @@ ALU = mybir.AluOpType
 
 P = 128
 PACK = 4
-PAIR = 2
 ROWS = D // PACK
 HALF = 128
 HALVES = M // HALF
-WIDTH = N // 2
 RUN = 4
 W, U = 0, 1
-EARLY, LATE = 0, WIDTH
+PAD = 256
 
 
 def tile_rows_gglu_tanh_bias_kernel(tc, x, w_words, w_scales, u_words, u_scales, b, out):
@@ -36,21 +34,25 @@ def tile_rows_gglu_tanh_bias_kernel(tc, x, w_words, w_scales, u_words, u_scales,
         psum = ctx.enter_context(tc.psum_pool(name="psum", bufs=1))
         ctx.enter_context(tc.manual_schedule())
 
-        words = [keep.tile([P, 2 * M], U8, align_bytes=64, name=f"words{k}") for k in range(2)]
-        planes = [keep.tile([P, M], U8, align_bytes=64, name=f"plane{k}") for k in range(2)]
-        bias_rows = keep.tile([P, G * HALVES, 32], F32, align_bytes=64)
-        bias = keep.tile([P, G * HALVES, 32], F32, align_bytes=64)
-        left = [keep.tile([P, PAIR, WIDTH], F32, name=f"left{r}") for r in range(2)]
-        right = keep.tile([P, PACK, WIDTH], F32)
-        grouped = keep.tile([P, N, PACK], BF16, align_bytes=64)
-        codes = keep.tile([P, WIDTH + N], U32, align_bytes=64)
-        scales = keep.tile([P, WIDTH + N], U8, align_bytes=64)
+        words = [keep.tile([P, 2 * M], U8, align_bytes=256, name=f"words{k}") for k in range(2)]
+        planes = [keep.tile([P, M], U8, align_bytes=256, name=f"plane{k}") for k in range(2)]
+        bias_rows = keep.tile([P, G * HALVES, 32], F32, align_bytes=256)
+        bias = keep.tile([P, G * HALVES, 32], F32, align_bytes=256)
+        grouped = keep.tile([P, N, PACK], BF16, align_bytes=256)
+        codes = keep.tile([P, PAD + N], U32, align_bytes=256)
+        scales = keep.tile([P, PAD + N], U8, align_bytes=256)
         banks = {}
         for h in range(HALVES):
             for k in range(2):
                 for g in range(G):
                     banks[h, k, g] = psum.tile([HALF, N], F32, name=f"bank{h}{k}{g}")
         gates = {}
+        filled = {}
+
+        def load_x(lo, hi, j0=0, j1=PACK):
+            raw = keep.tile([P, j1 - j0, hi - lo], F32, align_bytes=256, name=f"raw{lo}_{j0}")
+            nc.sync.dma_start(out=raw[:], in_=x_rows[:, j0:j1, lo:hi])
+            return raw, lo, j0, j1
 
         def load_words(k, source):
             nc.sync.dma_start(out=words[k][:].bitcast(I32), in_=source.rearrange("g p c -> (g p) c").bitcast(I32))
@@ -60,105 +62,116 @@ def tile_rows_gglu_tanh_bias_kernel(tc, x, w_words, w_scales, u_words, u_scales,
             for q in quadrants:
                 nc.sync.dma_start(out=planes[k][32 * q : 32 * q + 4, :].bitcast(I32), in_=rows[4 * q : 4 * q + 4, :])
 
-        def interleave_left(engine_copy, r, lo, hi):
-            engine_copy(
-                out=grouped[:, lo:hi, PAIR * r : PAIR * (r + 1)],
-                in_=left[r][:, :, lo:hi].rearrange("p j n -> p n j"),
-            )
+        def load_bias():
+            nc.sync.dma_start(out=bias_rows[0:P:32, :, :], in_=b.rearrange("g (h q j) o -> q (g h) (j o)", q=4, j=32))
 
-        def interleave_right(engine_copy, lo, hi):
-            engine_copy(
-                out=grouped[:, WIDTH + lo : WIDTH + hi, :].rearrange("p (c i) j -> p c j i", i=RUN),
-                in_=right[:, :, lo:hi].rearrange("p j (c i) -> p c j i", i=RUN),
-            )
+        def turn_bias():
+            nc.vector.transpose(out=bias[:].rearrange("p c j -> p (c j)"), in_=bias_rows[:].rearrange("p c j -> p (c j)"))
+
+        def interleave(engine_copy, chunk, lo, hi):
+            raw, first, j0, j1 = chunk
+            if j1 - j0 == PACK:
+                engine_copy(
+                    out=grouped[:, lo:hi, :].rearrange("p (c i) j -> p c j i", i=RUN),
+                    in_=raw[:, :, lo - first : hi - first].rearrange("p j (c i) -> p c j i", i=RUN),
+                )
+            else:
+                engine_copy(out=grouped[:, lo:hi, j0:j1], in_=raw[:, :, lo - first : hi - first].rearrange("p j n -> p n j"))
 
         def quantize(lo, hi):
             nc.vector.quantize_mx(
-                out=codes[:, WIDTH + lo : WIDTH + hi].bitcast(FP8X4),
-                scales=scales[:, WIDTH + lo : WIDTH + hi],
+                out=codes[:, PAD + lo : PAD + hi].bitcast(FP8X4),
+                scales=scales[:, PAD + lo : PAD + hi],
                 in_=grouped[:, lo:hi, :].rearrange("p n j -> p (n j)"),
             )
 
-        def multiply(g, k, h, first):
+        def multiply(g, k, h, ready):
             rows = slice(ROWS * g, ROWS * (g + 1))
+            window = slice(PAD + ready - N, PAD + ready)
+            filled[h, k, g] = ready
             nc.tensor.matmul_mx(
                 out=banks[h, k, g][:],
                 lhsT=words[k][rows, 2 * HALF * h : 2 * HALF * (h + 1)].bitcast(FP4X4),
                 lhsT_scale=planes[k][rows, HALF * h : HALF * (h + 1)],
-                rhs=codes[rows, first : first + N].bitcast(FP8X4),
-                rhs_scale=scales[rows, first : first + N],
+                rhs=codes[rows, window].bitcast(FP8X4),
+                rhs_scale=scales[rows, window],
                 start=True,
                 stop=True,
             )
 
-        def bank_columns(c, first):
-            return slice(WIDTH * (c + 1) - first, WIDTH * (c + 2) - first)
+        def sums(g, k, h, lo, hi):
+            shift = N - filled[h, k, g]
+            return banks[h, k, g][:, lo + shift : hi + shift]
 
-        def activate(g, h, c, first):
-            gates[g, h, c] = keep.tile([P, WIDTH], F32, name=f"gate{g}{h}{c}")
-            nc.scalar.activation(out=gates[g, h, c][:], in_=banks[h, W, g][:, bank_columns(c, first)], func=ACT.Tanh, bias=bias[:, g * HALVES + h, 0:1])
+        def activate(g, h, lo, hi):
+            gates[g, h, lo] = keep.tile([P, hi - lo], F32, align_bytes=256, name=f"gate{g}{h}_{lo}")
+            nc.scalar.activation(out=gates[g, h, lo][:], in_=sums(g, W, h, lo, hi), func=ACT.Tanh, bias=bias[:, g * HALVES + h, 0:1])
 
-        def gate_and_store(g, h, c, first):
-            result = keep.tile([P, WIDTH], F32, name=f"result{g}{h}{c}")
-            nc.vector.tensor_tensor(out=result[:], in0=banks[h, U, g][:, bank_columns(c, first)], in1=gates[g, h, c][:], op=ALU.mult)
-            nc.sync.dma_start(out=out[g, HALF * h : HALF * (h + 1), WIDTH * c : WIDTH * (c + 1)], in_=result[:])
+        def gate_and_store(g, h, lo, hi):
+            result = keep.tile([P, hi - lo], F32, align_bytes=256, name=f"result{g}{h}_{lo}")
+            nc.vector.tensor_tensor(out=result[:], in0=sums(g, U, h, lo, hi), in1=gates[g, h, lo][:], op=ALU.mult)
+            nc.sync.dma_start(out=out[g, HALF * h : HALF * (h + 1), lo:hi], in_=result[:])
+
+        vcopy, scopy = nc.vector.tensor_copy, nc.scalar.copy
 
         nc.vector.memset(planes[W][:].bitcast(I32), 0)
         nc.vector.memset(planes[U][:].bitcast(I32), 0)
         nc.vector.memset(bias_rows[:], 0.0)
-        nc.vector.memset(codes[:, :WIDTH], 0)
-        nc.vector.memset(scales[:, :WIDTH].bitcast(I32), 0)
+        nc.vector.memset(codes[:, :PAD], 0)
+        nc.vector.memset(scales[:, :PAD].bitcast(I32), 0)
 
-        for r in range(2):
-            nc.sync.dma_start(out=left[r][:], in_=x_rows[:, PAIR * r : PAIR * (r + 1), :WIDTH])
+        first = load_x(0, 128)
+        second = load_x(128, 256)
         load_words(W, w_words)
         load_plane(W, w_scales, (0, 1, 2, 3))
-        nc.sync.dma_start(out=right[:], in_=x_rows[:, :, WIDTH:])
-        nc.sync.dma_start(out=bias_rows[0:P:32, :, :], in_=b.rearrange("g (h q j) o -> q (g h) (j o)", q=4, j=32))
+        right = load_x(256, 512)
+        load_bias()
         load_words(U, u_words)
         load_plane(U, u_scales, (2, 3, 0, 1))
 
-        interleave_left(nc.scalar.copy, 0, 128, 256)
-        interleave_left(nc.vector.tensor_copy, 0, 0, 128)
-        interleave_left(nc.scalar.copy, 1, 176, 256)
-        interleave_left(nc.vector.tensor_copy, 1, 0, 128)
-        interleave_left(nc.vector.tensor_copy, 1, 128, 176)
-        quantize(0, 128)
-        quantize(128, 256)
-
-        interleave_right(nc.scalar.copy, 176, 256)
-        interleave_right(nc.vector.tensor_copy, 0, 128)
-        interleave_right(nc.vector.tensor_copy, 128, 176)
-        nc.vector.transpose(out=bias[:].rearrange("p c j -> p (c j)"), in_=bias_rows[:].rearrange("p c j -> p (c j)"))
+        interleave(scopy, first, 88, 128)
+        interleave(vcopy, first, 0, 64)
+        interleave(vcopy, first, 64, 88)
+        quantize(0, 64)
+        quantize(64, 128)
+        interleave(scopy, second, 216, 256)
+        interleave(vcopy, second, 128, 192)
+        interleave(vcopy, second, 192, 216)
+        quantize(128, 192)
+        quantize(192, 256)
+        interleave(scopy, right, 432, 512)
+        interleave(vcopy, right, 256, 384)
+        interleave(vcopy, right, 384, 432)
+        turn_bias()
         quantize(256, 384)
         quantize(384, 512)
 
-        multiply(0, W, 0, EARLY)
-        multiply(1, W, 0, EARLY)
-        multiply(0, W, 1, EARLY)
-        multiply(1, U, 0, EARLY)
-        multiply(0, U, 0, EARLY)
-        activate(1, 0, 0, EARLY)
-        activate(0, 0, 0, EARLY)
-        activate(0, 1, 0, EARLY)
-        gate_and_store(1, 0, 0, EARLY)
-        gate_and_store(0, 0, 0, EARLY)
+        multiply(0, W, 0, 256)
+        multiply(1, W, 0, 256)
+        multiply(0, W, 1, 256)
+        multiply(1, U, 0, 256)
+        multiply(0, U, 0, 256)
+        activate(1, 0, 0, 256)
+        activate(0, 0, 0, 256)
+        activate(0, 1, 0, 256)
+        gate_and_store(1, 0, 0, 256)
+        gate_and_store(0, 0, 0, 256)
 
-        multiply(1, W, 1, LATE)
-        multiply(0, U, 1, LATE)
-        multiply(1, U, 1, LATE)
-        multiply(0, W, 1, LATE)
-        activate(1, 1, 0, LATE)
-        activate(1, 1, 1, LATE)
-        activate(0, 1, 1, LATE)
-        gate_and_store(0, 1, 0, LATE)
-        gate_and_store(1, 1, 0, LATE)
-        gate_and_store(1, 1, 1, LATE)
-        gate_and_store(0, 1, 1, LATE)
+        multiply(1, W, 1, N)
+        multiply(0, U, 1, N)
+        multiply(1, U, 1, N)
+        multiply(0, W, 1, N)
+        activate(1, 1, 0, 256)
+        activate(1, 1, 256, N)
+        activate(0, 1, 256, N)
+        gate_and_store(0, 1, 0, 256)
+        gate_and_store(1, 1, 0, 256)
+        gate_and_store(1, 1, 256, N)
+        gate_and_store(0, 1, 256, N)
 
         for k in (W, U):
             for g in (1, 0):
-                multiply(g, k, 0, LATE)
+                multiply(g, k, 0, N)
         for g in (1, 0):
-            activate(g, 0, 1, LATE)
-            gate_and_store(g, 0, 1, LATE)
+            activate(g, 0, 256, N)
+            gate_and_store(g, 0, 256, N)

@@ -23,6 +23,7 @@ HALVES = M // HALF
 RUN = 4
 W, U = 0, 1
 PAD = 256
+BANKS = 4
 
 
 def tile_rows_gglu_tanh_bias_kernel(tc, x, w_words, w_scales, u_words, u_scales, b, out):
@@ -41,13 +42,9 @@ def tile_rows_gglu_tanh_bias_kernel(tc, x, w_words, w_scales, u_words, u_scales,
         grouped = keep.tile([P, N, PACK], BF16, align_bytes=256)
         codes = keep.tile([P, PAD + N], U32, align_bytes=256)
         scales = keep.tile([P, PAD + N], U8, align_bytes=256)
-        banks = {}
-        for h in range(HALVES):
-            for k in range(2):
-                for g in range(G):
-                    banks[h, k, g] = psum.tile([HALF, N], F32, name=f"bank{h}{k}{g}")
+        banks = [[psum.tile([HALF, N], F32, name=f"bank{g}{i}") for i in range(BANKS)] for g in range(G)]
         gates = {}
-        filled = {}
+        sums = {}
 
         def load_x(lo, hi, j0=0, j1=PACK):
             raw = keep.tile([P, j1 - j0, hi - lo], F32, align_bytes=256, name=f"raw{lo}_{j0}")
@@ -57,9 +54,9 @@ def tile_rows_gglu_tanh_bias_kernel(tc, x, w_words, w_scales, u_words, u_scales,
         def load_words(k, source):
             nc.sync.dma_start(out=words[k][:].bitcast(I32), in_=source.rearrange("g p c -> (g p) c").bitcast(I32))
 
-        def load_plane(k, source, quadrants):
+        def load_plane(k, source, g):
             rows = source.rearrange("g f m -> (g f) m").bitcast(I32)
-            for q in quadrants:
+            for q in (2 * g, 2 * g + 1):
                 nc.sync.dma_start(out=planes[k][32 * q : 32 * q + 4, :].bitcast(I32), in_=rows[4 * q : 4 * q + 4, :])
 
         def load_bias():
@@ -85,12 +82,12 @@ def tile_rows_gglu_tanh_bias_kernel(tc, x, w_words, w_scales, u_words, u_scales,
                 in_=grouped[:, lo:hi, :].rearrange("p n j -> p (n j)"),
             )
 
-        def multiply(g, k, h, ready):
+        def multiply(g, k, h, ready, bank):
             rows = slice(ROWS * g, ROWS * (g + 1))
             window = slice(PAD + ready - N, PAD + ready)
-            filled[h, k, g] = ready
+            sums[g, k, h, ready] = banks[g][bank]
             nc.tensor.matmul_mx(
-                out=banks[h, k, g][:],
+                out=banks[g][bank][:],
                 lhsT=words[k][rows, 2 * HALF * h : 2 * HALF * (h + 1)].bitcast(FP4X4),
                 lhsT_scale=planes[k][rows, HALF * h : HALF * (h + 1)],
                 rhs=codes[rows, window].bitcast(FP8X4),
@@ -99,17 +96,16 @@ def tile_rows_gglu_tanh_bias_kernel(tc, x, w_words, w_scales, u_words, u_scales,
                 stop=True,
             )
 
-        def sums(g, k, h, lo, hi):
-            shift = N - filled[h, k, g]
-            return banks[h, k, g][:, lo + shift : hi + shift]
+        def columns(g, k, h, ready, lo, hi):
+            return sums[g, k, h, ready][:, lo + N - ready : hi + N - ready]
 
-        def activate(g, h, lo, hi):
+        def activate(g, h, ready, lo, hi):
             gates[g, h, lo] = keep.tile([P, hi - lo], F32, align_bytes=256, name=f"gate{g}{h}_{lo}")
-            nc.scalar.activation(out=gates[g, h, lo][:], in_=sums(g, W, h, lo, hi), func=ACT.Tanh, bias=bias[:, g * HALVES + h, 0:1])
+            nc.scalar.activation(out=gates[g, h, lo][:], in_=columns(g, W, h, ready, lo, hi), func=ACT.Tanh, bias=bias[:, g * HALVES + h, 0:1])
 
-        def gate_and_store(g, h, lo, hi):
+        def gate_and_store(g, h, ready, lo, hi):
             result = keep.tile([P, hi - lo], F32, align_bytes=256, name=f"result{g}{h}_{lo}")
-            nc.vector.tensor_tensor(out=result[:], in0=sums(g, U, h, lo, hi), in1=gates[g, h, lo][:], op=ALU.mult)
+            nc.vector.tensor_tensor(out=result[:], in0=columns(g, U, h, ready, lo, hi), in1=gates[g, h, lo][:], op=ALU.mult)
             nc.sync.dma_start(out=out[g, HALF * h : HALF * (h + 1), lo:hi], in_=result[:])
 
         vcopy, scopy = nc.vector.tensor_copy, nc.scalar.copy
@@ -123,11 +119,13 @@ def tile_rows_gglu_tanh_bias_kernel(tc, x, w_words, w_scales, u_words, u_scales,
         first = load_x(0, 128)
         second = load_x(128, 256)
         load_words(W, w_words)
-        load_plane(W, w_scales, (0, 1, 2, 3))
+        load_plane(W, w_scales, 0)
+        load_plane(W, w_scales, 1)
         right = load_x(256, 512)
         load_bias()
         load_words(U, u_words)
-        load_plane(U, u_scales, (2, 3, 0, 1))
+        load_plane(U, u_scales, 1)
+        load_plane(U, u_scales, 0)
 
         interleave(scopy, first, 88, 128)
         interleave(vcopy, first, 0, 64)
@@ -141,37 +139,38 @@ def tile_rows_gglu_tanh_bias_kernel(tc, x, w_words, w_scales, u_words, u_scales,
         quantize(192, 256)
         interleave(scopy, right, 432, 512)
         interleave(vcopy, right, 256, 384)
-        interleave(vcopy, right, 384, 432)
         turn_bias()
+        interleave(vcopy, right, 384, 432)
         quantize(256, 384)
         quantize(384, 512)
 
-        multiply(0, W, 0, 256)
-        multiply(1, W, 0, 256)
-        multiply(0, W, 1, 256)
-        multiply(1, U, 0, 256)
-        multiply(0, U, 0, 256)
-        activate(1, 0, 0, 256)
-        activate(0, 0, 0, 256)
-        activate(0, 1, 0, 256)
-        gate_and_store(1, 0, 0, 256)
-        gate_and_store(0, 0, 0, 256)
-
-        multiply(1, W, 1, N)
-        multiply(0, U, 1, N)
-        multiply(1, U, 1, N)
-        multiply(0, W, 1, N)
-        activate(1, 1, 0, 256)
-        activate(1, 1, 256, N)
-        activate(0, 1, 256, N)
-        gate_and_store(0, 1, 0, 256)
-        gate_and_store(1, 1, 0, 256)
-        gate_and_store(1, 1, 256, N)
-        gate_and_store(0, 1, 256, N)
-
-        for k in (W, U):
-            for g in (1, 0):
-                multiply(g, k, 0, N)
-        for g in (1, 0):
-            activate(g, 0, 256, N)
-            gate_and_store(g, 0, 256, N)
+        multiply(1, W, 0, 256, 0)
+        multiply(0, W, 0, 256, 0)
+        multiply(1, W, 1, 256, 1)
+        multiply(0, W, 1, 256, 1)
+        multiply(1, U, 0, 256, 2)
+        multiply(0, U, 0, 256, 2)
+        activate(1, 0, 256, 0, 256)
+        activate(0, 0, 256, 0, 256)
+        activate(0, 1, 256, 0, 256)
+        activate(1, 1, 256, 0, 256)
+        gate_and_store(1, 0, 256, 0, 256)
+        gate_and_store(0, 0, 256, 0, 256)
+        multiply(1, W, 1, 512, 3)
+        multiply(0, U, 1, 512, 3)
+        multiply(1, U, 1, 512, 0)
+        multiply(0, W, 1, 512, 0)
+        activate(1, 1, 512, 256, 512)
+        activate(0, 1, 512, 256, 512)
+        multiply(1, W, 0, 512, 1)
+        multiply(0, W, 0, 512, 1)
+        multiply(1, U, 0, 512, 2)
+        multiply(0, U, 0, 512, 2)
+        gate_and_store(0, 1, 512, 0, 256)
+        gate_and_store(1, 1, 512, 0, 256)
+        gate_and_store(1, 1, 512, 256, 512)
+        gate_and_store(0, 1, 512, 256, 512)
+        activate(1, 0, 512, 256, 512)
+        activate(0, 0, 512, 256, 512)
+        gate_and_store(1, 0, 512, 256, 512)
+        gate_and_store(0, 0, 512, 256, 512)

@@ -22,7 +22,7 @@ HALF = 128
 HALVES = M // HALF
 RUN = 4
 W, U = 0, 1
-PAD = 256
+PAD = 384
 BANKS = 4
 
 
@@ -43,7 +43,8 @@ def tile_rows_gglu_tanh_bias_kernel(tc, x, w_words, w_scales, u_words, u_scales,
         codes = keep.tile([P, PAD + N], U32, align_bytes=256)
         scales = keep.tile([P, PAD + N], U8, align_bytes=256)
         banks = [[psum.tile([HALF, N], F32, name=f"bank{g}{i}") for i in range(BANKS)] for g in range(G)]
-        gates = {}
+        gates = [[keep.tile([P, N], F32, align_bytes=256, name=f"gate{g}{h}") for h in range(HALVES)] for g in range(G)]
+        results = [[keep.tile([P, N], F32, align_bytes=256, name=f"result{g}{h}") for h in range(HALVES)] for g in range(G)]
         sums = {}
 
         def load_x(lo, hi, j0=0, j1=PACK):
@@ -51,16 +52,16 @@ def tile_rows_gglu_tanh_bias_kernel(tc, x, w_words, w_scales, u_words, u_scales,
             nc.sync.dma_start(out=raw[:], in_=x_rows[:, j0:j1, lo:hi])
             return raw, lo, j0, j1
 
-        def load_words(k, source):
-            nc.sync.dma_start(out=words[k][:].bitcast(I32), in_=source.rearrange("g p c -> (g p) c").bitcast(I32))
+        def load_words(k, source, queue=nc.sync):
+            queue.dma_start(out=words[k][:].bitcast(I32), in_=source.rearrange("g p c -> (g p) c").bitcast(I32))
 
-        def load_plane(k, source, g):
+        def load_plane(k, source, quadrants, queue=nc.sync):
             rows = source.rearrange("g f m -> (g f) m").bitcast(I32)
-            for q in (2 * g, 2 * g + 1):
-                nc.sync.dma_start(out=planes[k][32 * q : 32 * q + 4, :].bitcast(I32), in_=rows[4 * q : 4 * q + 4, :])
+            for q in quadrants:
+                queue.dma_start(out=planes[k][32 * q : 32 * q + 4, :].bitcast(I32), in_=rows[4 * q : 4 * q + 4, :])
 
-        def load_bias():
-            nc.sync.dma_start(out=bias_rows[0:P:32, :, :], in_=b.rearrange("g (h q j) o -> q (g h) (j o)", q=4, j=32))
+        def load_bias(queue=nc.sync):
+            queue.dma_start(out=bias_rows[0:P:32, :, :], in_=b.rearrange("g (h q j) o -> q (g h) (j o)", q=4, j=32))
 
         def turn_bias():
             nc.vector.transpose(out=bias[:].rearrange("p c j -> p (c j)"), in_=bias_rows[:].rearrange("p c j -> p (c j)"))
@@ -100,15 +101,20 @@ def tile_rows_gglu_tanh_bias_kernel(tc, x, w_words, w_scales, u_words, u_scales,
             return sums[g, k, h, ready][:, lo + N - ready : hi + N - ready]
 
         def activate(g, h, ready, lo, hi):
-            gates[g, h, lo] = keep.tile([P, hi - lo], F32, align_bytes=256, name=f"gate{g}{h}_{lo}")
-            nc.scalar.activation(out=gates[g, h, lo][:], in_=columns(g, W, h, ready, lo, hi), func=ACT.Tanh, bias=bias[:, g * HALVES + h, 0:1])
+            nc.scalar.activation(out=gates[g][h][:, lo:hi], in_=columns(g, W, h, ready, lo, hi), func=ACT.Tanh, bias=bias[:, g * HALVES + h, 0:1])
+
+        def gate(g, h, ready, lo, hi):
+            nc.vector.tensor_tensor(out=results[g][h][:, lo:hi], in0=columns(g, U, h, ready, lo, hi), in1=gates[g][h][:, lo:hi], op=ALU.mult)
+
+        def store(g, h, lo, hi):
+            nc.sync.dma_start(out=out[g, HALF * h : HALF * (h + 1), lo:hi], in_=results[g][h][:, lo:hi])
 
         def gate_and_store(g, h, ready, lo, hi):
-            result = keep.tile([P, hi - lo], F32, align_bytes=256, name=f"result{g}{h}_{lo}")
-            nc.vector.tensor_tensor(out=result[:], in0=columns(g, U, h, ready, lo, hi), in1=gates[g, h, lo][:], op=ALU.mult)
-            nc.sync.dma_start(out=out[g, HALF * h : HALF * (h + 1), lo:hi], in_=result[:])
+            gate(g, h, ready, lo, hi)
+            store(g, h, lo, hi)
 
         vcopy, scopy = nc.vector.tensor_copy, nc.scalar.copy
+        sync, scalar = nc.sync, nc.scalar
 
         nc.vector.memset(planes[W][:].bitcast(I32), 0)
         nc.vector.memset(planes[U][:].bitcast(I32), 0)
@@ -119,39 +125,43 @@ def tile_rows_gglu_tanh_bias_kernel(tc, x, w_words, w_scales, u_words, u_scales,
         first = load_x(0, 128)
         second = load_x(128, 256)
         load_words(W, w_words)
-        load_plane(W, w_scales, 0)
-        load_plane(W, w_scales, 1)
+        load_plane(W, w_scales, (0, 1))
+        load_plane(W, w_scales, (2, 3))
         right = load_x(256, 512)
-        load_bias()
-        load_words(U, u_words)
-        load_plane(U, u_scales, 1)
-        load_plane(U, u_scales, 0)
-
         interleave(scopy, first, 88, 128)
+        load_bias(scalar)
         interleave(vcopy, first, 0, 64)
         interleave(vcopy, first, 64, 88)
         quantize(0, 64)
         quantize(64, 128)
         interleave(scopy, second, 216, 256)
+        load_words(U, u_words)
+        load_plane(U, u_scales, (2,), scalar)
+        load_plane(U, u_scales, (3,), sync)
+        load_plane(U, u_scales, (0,), scalar)
+        load_plane(U, u_scales, (1,), sync)
+        multiply(1, W, 0, 128, 3)
+        multiply(0, W, 0, 128, 3)
         interleave(vcopy, second, 128, 192)
         interleave(vcopy, second, 192, 216)
         quantize(128, 192)
         quantize(192, 256)
+        turn_bias()
         interleave(scopy, right, 432, 512)
         interleave(vcopy, right, 256, 384)
-        turn_bias()
         interleave(vcopy, right, 384, 432)
         quantize(256, 384)
         quantize(384, 512)
-
         multiply(1, W, 0, 256, 0)
         multiply(0, W, 0, 256, 0)
         multiply(1, W, 1, 256, 1)
         multiply(0, W, 1, 256, 1)
         multiply(1, U, 0, 256, 2)
         multiply(0, U, 0, 256, 2)
-        activate(1, 0, 256, 0, 256)
-        activate(0, 0, 256, 0, 256)
+        activate(1, 0, 128, 0, 128)
+        activate(1, 0, 256, 128, 256)
+        activate(0, 0, 128, 0, 128)
+        activate(0, 0, 256, 128, 256)
         activate(0, 1, 256, 0, 256)
         activate(1, 1, 256, 0, 256)
         gate_and_store(1, 0, 256, 0, 256)

@@ -128,55 +128,57 @@ def tile_rows_gglu_tanh_bias_kernel(tc, x, w_words, w_scales, u_words, u_scales,
         load_plane(W, w_scales, (0, 1))
         load_plane(W, w_scales, (2, 3))
         right = load_x(256, 512)
+        load_bias()
+        load_words(U, u_words)
+        load_plane(U, u_scales, (2, 3))
+        load_plane(U, u_scales, (0, 1))
         interleave(scopy, first, 88, 128)
-        load_bias(scalar)
         interleave(vcopy, first, 0, 64)
         interleave(vcopy, first, 64, 88)
         quantize(0, 64)
         quantize(64, 128)
         interleave(scopy, second, 216, 256)
-        load_words(U, u_words)
-        load_plane(U, u_scales, (2,), scalar)
-        load_plane(U, u_scales, (3,), sync)
-        load_plane(U, u_scales, (0,), scalar)
-        load_plane(U, u_scales, (1,), sync)
-        multiply(1, W, 0, 128, 3)
-        multiply(0, W, 0, 128, 3)
         interleave(vcopy, second, 128, 192)
         interleave(vcopy, second, 192, 216)
         quantize(128, 192)
         quantize(192, 256)
-        turn_bias()
-        interleave(scopy, right, 432, 512)
-        interleave(vcopy, right, 256, 384)
-        interleave(vcopy, right, 384, 432)
-        quantize(256, 384)
-        quantize(384, 512)
-        multiply(1, W, 0, 256, 0)
-        multiply(0, W, 0, 256, 0)
-        multiply(1, W, 1, 256, 1)
-        multiply(0, W, 1, 256, 1)
+        multiply(1, W, 0, 128, 0)
+        multiply(0, W, 0, 128, 0)
+        multiply(1, W, 0, 256, 1)
+        multiply(0, W, 0, 256, 1)
+        multiply(0, W, 1, 256, 2)
         multiply(1, U, 0, 256, 2)
-        multiply(0, U, 0, 256, 2)
+        multiply(1, W, 1, 256, 3)
+        multiply(0, U, 0, 256, 3)
+        interleave(scopy, right, 448, 512)
+        interleave(scopy, right, 432, 448)
+        interleave(vcopy, right, 256, 320)
+        turn_bias()
+        interleave(vcopy, right, 320, 384)
+        interleave(vcopy, right, 384, 432)
+        quantize(256, 320)
+        quantize(448, 512)
+        quantize(320, 384)
+        quantize(384, 448)
         activate(1, 0, 128, 0, 128)
-        activate(1, 0, 256, 128, 256)
         activate(0, 0, 128, 0, 128)
+        activate(1, 0, 256, 128, 256)
         activate(0, 0, 256, 128, 256)
         activate(0, 1, 256, 0, 256)
-        activate(1, 1, 256, 0, 256)
         gate_and_store(1, 0, 256, 0, 256)
+        activate(1, 1, 256, 0, 256)
         gate_and_store(0, 0, 256, 0, 256)
-        multiply(1, W, 1, 512, 3)
-        multiply(0, U, 1, 512, 3)
-        multiply(1, U, 1, 512, 0)
-        multiply(0, W, 1, 512, 0)
+        multiply(0, U, 1, 512, 0)
+        multiply(1, W, 1, 512, 0)
+        multiply(1, U, 1, 512, 1)
+        multiply(0, W, 1, 512, 1)
+        gate_and_store(0, 1, 512, 0, 256)
         activate(1, 1, 512, 256, 512)
         activate(0, 1, 512, 256, 512)
-        multiply(1, W, 0, 512, 1)
-        multiply(0, W, 0, 512, 1)
-        multiply(1, U, 0, 512, 2)
-        multiply(0, U, 0, 512, 2)
-        gate_and_store(0, 1, 512, 0, 256)
+        multiply(0, W, 0, 512, 2)
+        multiply(1, W, 0, 512, 2)
+        multiply(1, U, 0, 512, 3)
+        multiply(0, U, 0, 512, 3)
         gate_and_store(1, 1, 512, 0, 256)
         gate_and_store(1, 1, 512, 256, 512)
         gate_and_store(0, 1, 512, 256, 512)

@@ -22,7 +22,8 @@ HALF = 128
 HALVES = M // HALF
 RUN = 4
 W, U = 0, 1
-PAD = 384
+PAD = 512
+FIRST = 128
 BANKS = 4
 
 
@@ -119,19 +120,23 @@ def tile_rows_gglu_tanh_bias_kernel(tc, x, w_words, w_scales, u_words, u_scales,
         nc.vector.memset(planes[W][:].bitcast(I32), 0)
         nc.vector.memset(planes[U][:].bitcast(I32), 0)
         nc.vector.memset(bias_rows[:], 0.0)
-        nc.vector.memset(codes[:, :PAD], 0)
-        nc.vector.memset(scales[:, :PAD].bitcast(I32), 0)
+        nc.vector.memset(codes[:, FIRST:PAD], 0)
+        nc.vector.memset(scales[:, FIRST:PAD].bitcast(I32), 0)
 
         first = load_x(0, 128)
         second = load_x(128, 256)
+        load_plane(W, w_scales, (2,), sync)
+        load_plane(W, w_scales, (3,), sync)
         load_words(W, w_words)
-        load_plane(W, w_scales, (0, 1))
-        load_plane(W, w_scales, (2, 3))
+        load_plane(W, w_scales, (0,), sync)
+        load_plane(W, w_scales, (1,), sync)
         right = load_x(256, 512)
         load_bias()
         load_words(U, u_words)
-        load_plane(U, u_scales, (2, 3))
-        load_plane(U, u_scales, (0, 1))
+        load_plane(U, u_scales, (2,), sync)
+        load_plane(U, u_scales, (3,), sync)
+        load_plane(U, u_scales, (0,), sync)
+        load_plane(U, u_scales, (1,), sync)
         interleave(scopy, first, 88, 128)
         interleave(vcopy, first, 0, 64)
         interleave(vcopy, first, 64, 88)
@@ -146,16 +151,16 @@ def tile_rows_gglu_tanh_bias_kernel(tc, x, w_words, w_scales, u_words, u_scales,
         multiply(0, W, 0, 128, 0)
         multiply(1, W, 0, 256, 1)
         multiply(0, W, 0, 256, 1)
+        multiply(1, W, 1, 256, 2)
         multiply(0, W, 1, 256, 2)
-        multiply(1, U, 0, 256, 2)
-        multiply(1, W, 1, 256, 3)
+        multiply(1, U, 0, 256, 3)
         multiply(0, U, 0, 256, 3)
         interleave(scopy, right, 448, 512)
-        interleave(scopy, right, 432, 448)
+        interleave(scopy, right, 416, 448)
         interleave(vcopy, right, 256, 320)
         turn_bias()
         interleave(vcopy, right, 320, 384)
-        interleave(vcopy, right, 384, 432)
+        interleave(vcopy, right, 384, 416)
         quantize(256, 320)
         quantize(448, 512)
         quantize(320, 384)
@@ -164,25 +169,25 @@ def tile_rows_gglu_tanh_bias_kernel(tc, x, w_words, w_scales, u_words, u_scales,
         activate(0, 0, 128, 0, 128)
         activate(1, 0, 256, 128, 256)
         activate(0, 0, 256, 128, 256)
+        activate(1, 1, 256, 0, 256)
         activate(0, 1, 256, 0, 256)
         gate_and_store(1, 0, 256, 0, 256)
-        activate(1, 1, 256, 0, 256)
         gate_and_store(0, 0, 256, 0, 256)
         multiply(0, U, 1, 512, 0)
         multiply(1, W, 1, 512, 0)
-        multiply(1, U, 1, 512, 1)
         multiply(0, W, 1, 512, 1)
-        gate_and_store(0, 1, 512, 0, 256)
+        multiply(1, U, 1, 512, 1)
         activate(1, 1, 512, 256, 512)
+        gate_and_store(0, 1, 512, 0, 256)
         activate(0, 1, 512, 256, 512)
-        multiply(0, W, 0, 512, 2)
+        gate_and_store(1, 1, 512, 0, 256)
         multiply(1, W, 0, 512, 2)
+        multiply(0, W, 0, 512, 2)
+        gate_and_store(1, 1, 512, 256, 512)
+        activate(1, 0, 512, 256, 512)
+        gate_and_store(0, 1, 512, 256, 512)
         multiply(1, U, 0, 512, 3)
         multiply(0, U, 0, 512, 3)
-        gate_and_store(1, 1, 512, 0, 256)
-        gate_and_store(1, 1, 512, 256, 512)
-        gate_and_store(0, 1, 512, 256, 512)
-        activate(1, 0, 512, 256, 512)
-        activate(0, 0, 512, 256, 512)
         gate_and_store(1, 0, 512, 256, 512)
+        activate(0, 0, 512, 256, 512)
         gate_and_store(0, 0, 512, 256, 512)

@@ -125,7 +125,7 @@ def tile_rows_gglu_tanh_bias_kernel(tc, x, w_words, w_scales, u_words, u_scales,
 
         first = load_x(0, 128)
         second = load_x(128, 256)
-        load_plane(W, w_scales, (2,), sync)
+        load_plane(W, w_scales, (2,), scalar)
         load_plane(W, w_scales, (3,), sync)
         load_words(W, w_words)
         load_plane(W, w_scales, (0,), sync)
@@ -137,9 +137,8 @@ def tile_rows_gglu_tanh_bias_kernel(tc, x, w_words, w_scales, u_words, u_scales,
         load_plane(U, u_scales, (3,), sync)
         load_plane(U, u_scales, (0,), sync)
         load_plane(U, u_scales, (1,), sync)
-        interleave(scopy, first, 88, 128)
         interleave(vcopy, first, 0, 64)
-        interleave(vcopy, first, 64, 88)
+        interleave(vcopy, first, 64, 128)
         quantize(0, 64)
         quantize(64, 128)
         interleave(scopy, second, 216, 256)
@@ -151,9 +150,9 @@ def tile_rows_gglu_tanh_bias_kernel(tc, x, w_words, w_scales, u_words, u_scales,
         multiply(0, W, 0, 128, 0)
         multiply(1, W, 0, 256, 1)
         multiply(0, W, 0, 256, 1)
-        multiply(1, W, 1, 256, 2)
         multiply(0, W, 1, 256, 2)
-        multiply(1, U, 0, 256, 3)
+        multiply(1, U, 0, 256, 2)
+        multiply(1, W, 1, 256, 3)
         multiply(0, U, 0, 256, 3)
         interleave(scopy, right, 448, 512)
         interleave(scopy, right, 416, 448)
@@ -169,25 +168,25 @@ def tile_rows_gglu_tanh_bias_kernel(tc, x, w_words, w_scales, u_words, u_scales,
         activate(0, 0, 128, 0, 128)
         activate(1, 0, 256, 128, 256)
         activate(0, 0, 256, 128, 256)
-        activate(1, 1, 256, 0, 256)
         activate(0, 1, 256, 0, 256)
         gate_and_store(1, 0, 256, 0, 256)
+        activate(1, 1, 256, 0, 256)
         gate_and_store(0, 0, 256, 0, 256)
         multiply(0, U, 1, 512, 0)
         multiply(1, W, 1, 512, 0)
-        multiply(0, W, 1, 512, 1)
         multiply(1, U, 1, 512, 1)
-        activate(1, 1, 512, 256, 512)
+        multiply(0, W, 1, 512, 1)
         gate_and_store(0, 1, 512, 0, 256)
+        activate(1, 1, 512, 256, 512)
         activate(0, 1, 512, 256, 512)
-        gate_and_store(1, 1, 512, 0, 256)
-        multiply(1, W, 0, 512, 2)
         multiply(0, W, 0, 512, 2)
-        gate_and_store(1, 1, 512, 256, 512)
-        activate(1, 0, 512, 256, 512)
-        gate_and_store(0, 1, 512, 256, 512)
+        multiply(1, W, 0, 512, 2)
         multiply(1, U, 0, 512, 3)
         multiply(0, U, 0, 512, 3)
-        gate_and_store(1, 0, 512, 256, 512)
+        gate_and_store(1, 1, 512, 0, 256)
+        gate_and_store(1, 1, 512, 256, 512)
+        gate_and_store(0, 1, 512, 256, 512)
+        activate(1, 0, 512, 256, 512)
         activate(0, 0, 512, 256, 512)
+        gate_and_store(1, 0, 512, 256, 512)
         gate_and_store(0, 0, 512, 256, 512)

@@ -16,15 +16,22 @@ ACT = mybir.ActivationFunctionType
 ALU = mybir.AluOpType
 
 P = 128
+QUADRANT = 32
 PACK = 4
 ROWS = D // PACK
 HALF = 128
 HALVES = M // HALF
-RUN = 4
 W, U = 0, 1
-PAD = 512
-FIRST = 128
 BANKS = 4
+RUN = 4
+ALIGN = 256
+
+FIRST = 128
+LEFT = 256
+STEP = 64
+PAD = N
+SCALAR_FROM_LEFT = 216
+SCALAR_FROM_RIGHT = 416
 
 
 def tile_rows_gglu_tanh_bias_kernel(tc, x, w_words, w_scales, u_words, u_scales, b, out):
@@ -36,60 +43,55 @@ def tile_rows_gglu_tanh_bias_kernel(tc, x, w_words, w_scales, u_words, u_scales,
         psum = ctx.enter_context(tc.psum_pool(name="psum", bufs=1))
         ctx.enter_context(tc.manual_schedule())
 
-        words = [keep.tile([P, 2 * M], U8, align_bytes=256, name=f"words{k}") for k in range(2)]
-        planes = [keep.tile([P, M], U8, align_bytes=256, name=f"plane{k}") for k in range(2)]
-        bias_rows = keep.tile([P, G * HALVES, 32], F32, align_bytes=256)
-        bias = keep.tile([P, G * HALVES, 32], F32, align_bytes=256)
-        grouped = keep.tile([P, N, PACK], BF16, align_bytes=256)
-        codes = keep.tile([P, PAD + N], U32, align_bytes=256)
-        scales = keep.tile([P, PAD + N], U8, align_bytes=256)
+        words = [keep.tile([P, 2 * M], U8, align_bytes=ALIGN, name=f"words{k}") for k in (W, U)]
+        planes = [keep.tile([P, M], U8, align_bytes=ALIGN, name=f"plane{k}") for k in (W, U)]
+        bias_rows = keep.tile([P, G * HALVES, QUADRANT], F32, align_bytes=ALIGN)
+        bias = keep.tile([P, G * HALVES, QUADRANT], F32, align_bytes=ALIGN)
+        grouped = keep.tile([P, N, PACK], BF16, align_bytes=ALIGN)
+        codes = keep.tile([P, PAD + N], U32, align_bytes=ALIGN)
+        scales = keep.tile([P, PAD + N], U8, align_bytes=ALIGN)
         banks = [[psum.tile([HALF, N], F32, name=f"bank{g}{i}") for i in range(BANKS)] for g in range(G)]
-        gates = [[keep.tile([P, N], F32, align_bytes=256, name=f"gate{g}{h}") for h in range(HALVES)] for g in range(G)]
-        results = [[keep.tile([P, N], F32, align_bytes=256, name=f"result{g}{h}") for h in range(HALVES)] for g in range(G)]
-        sums = {}
+        gates = [[keep.tile([P, N], F32, align_bytes=ALIGN, name=f"gate{g}{h}") for h in range(HALVES)] for g in range(G)]
+        results = [[keep.tile([P, N], F32, align_bytes=ALIGN, name=f"result{g}{h}") for h in range(HALVES)] for g in range(G)]
+        passes = [[] for g in range(G)]
 
-        def load_x(lo, hi, j0=0, j1=PACK):
-            raw = keep.tile([P, j1 - j0, hi - lo], F32, align_bytes=256, name=f"raw{lo}_{j0}")
-            nc.sync.dma_start(out=raw[:], in_=x_rows[:, j0:j1, lo:hi])
-            return raw, lo, j0, j1
+        def load_x(lo, hi):
+            raw = keep.tile([P, PACK, hi - lo], F32, align_bytes=ALIGN, name=f"raw{lo}")
+            nc.sync.dma_start(out=raw[:], in_=x_rows[:, :, lo:hi])
+            return raw, lo
 
-        def load_words(k, source, queue=nc.sync):
-            queue.dma_start(out=words[k][:].bitcast(I32), in_=source.rearrange("g p c -> (g p) c").bitcast(I32))
+        def load_words(k, source):
+            nc.sync.dma_start(out=words[k][:].bitcast(I32), in_=source.rearrange("g p c -> (g p) c").bitcast(I32))
 
-        def load_plane(k, source, quadrants, queue=nc.sync):
+        def load_plane(k, source, q, queue):
             rows = source.rearrange("g f m -> (g f) m").bitcast(I32)
-            for q in quadrants:
-                queue.dma_start(out=planes[k][32 * q : 32 * q + 4, :].bitcast(I32), in_=rows[4 * q : 4 * q + 4, :])
+            queue.dma_start(out=planes[k][QUADRANT * q : QUADRANT * q + 4, :].bitcast(I32), in_=rows[4 * q : 4 * q + 4, :])
 
-        def load_bias(queue=nc.sync):
-            queue.dma_start(out=bias_rows[0:P:32, :, :], in_=b.rearrange("g (h q j) o -> q (g h) (j o)", q=4, j=32))
+        def load_bias():
+            nc.sync.dma_start(out=bias_rows[0:P:QUADRANT, :, :], in_=b.rearrange("g (h q j) o -> q (g h) (j o)", q=4, j=QUADRANT))
 
         def turn_bias():
             nc.vector.transpose(out=bias[:].rearrange("p c j -> p (c j)"), in_=bias_rows[:].rearrange("p c j -> p (c j)"))
 
-        def interleave(engine_copy, chunk, lo, hi):
-            raw, first, j0, j1 = chunk
-            if j1 - j0 == PACK:
-                engine_copy(
-                    out=grouped[:, lo:hi, :].rearrange("p (c i) j -> p c j i", i=RUN),
-                    in_=raw[:, :, lo - first : hi - first].rearrange("p j (c i) -> p c j i", i=RUN),
-                )
-            else:
-                engine_copy(out=grouped[:, lo:hi, j0:j1], in_=raw[:, :, lo - first : hi - first].rearrange("p j n -> p n j"))
-
-        def quantize(lo, hi):
-            nc.vector.quantize_mx(
-                out=codes[:, PAD + lo : PAD + hi].bitcast(FP8X4),
-                scales=scales[:, PAD + lo : PAD + hi],
-                in_=grouped[:, lo:hi, :].rearrange("p n j -> p (n j)"),
+        def interleave(copy, chunk, lo, hi):
+            raw, start = chunk
+            copy(
+                out=grouped[:, lo:hi, :].rearrange("p (c i) j -> p c j i", i=RUN),
+                in_=raw[:, :, lo - start : hi - start].rearrange("p j (c i) -> p c j i", i=RUN),
             )
 
-        def multiply(g, k, h, ready, bank):
+        def quantize(lo):
+            nc.vector.quantize_mx(
+                out=codes[:, PAD + lo : PAD + lo + STEP].bitcast(FP8X4),
+                scales=scales[:, PAD + lo : PAD + lo + STEP],
+                in_=grouped[:, lo : lo + STEP, :].rearrange("p n j -> p (n j)"),
+            )
+
+        def multiply(g, k, h, ready):
             rows = slice(ROWS * g, ROWS * (g + 1))
             window = slice(PAD + ready - N, PAD + ready)
-            sums[g, k, h, ready] = banks[g][bank]
             nc.tensor.matmul_mx(
-                out=banks[g][bank][:],
+                out=banks[g][len(passes[g]) % BANKS][:],
                 lhsT=words[k][rows, 2 * HALF * h : 2 * HALF * (h + 1)].bitcast(FP4X4),
                 lhsT_scale=planes[k][rows, HALF * h : HALF * (h + 1)],
                 rhs=codes[rows, window].bitcast(FP8X4),
@@ -97,96 +99,88 @@ def tile_rows_gglu_tanh_bias_kernel(tc, x, w_words, w_scales, u_words, u_scales,
                 start=True,
                 stop=True,
             )
+            passes[g].append((k, h, ready))
 
-        def columns(g, k, h, ready, lo, hi):
-            return sums[g, k, h, ready][:, lo + N - ready : hi + N - ready]
+        def sums(g, k, h, ready, lo, hi):
+            bank = banks[g][passes[g].index((k, h, ready)) % BANKS]
+            return bank[:, lo + N - ready : hi + N - ready]
 
         def activate(g, h, ready, lo, hi):
-            nc.scalar.activation(out=gates[g][h][:, lo:hi], in_=columns(g, W, h, ready, lo, hi), func=ACT.Tanh, bias=bias[:, g * HALVES + h, 0:1])
-
-        def gate(g, h, ready, lo, hi):
-            nc.vector.tensor_tensor(out=results[g][h][:, lo:hi], in0=columns(g, U, h, ready, lo, hi), in1=gates[g][h][:, lo:hi], op=ALU.mult)
-
-        def store(g, h, lo, hi):
-            nc.sync.dma_start(out=out[g, HALF * h : HALF * (h + 1), lo:hi], in_=results[g][h][:, lo:hi])
+            nc.scalar.activation(out=gates[g][h][:, lo:hi], in_=sums(g, W, h, ready, lo, hi), func=ACT.Tanh, bias=bias[:, g * HALVES + h, 0:1])
 
         def gate_and_store(g, h, ready, lo, hi):
-            gate(g, h, ready, lo, hi)
-            store(g, h, lo, hi)
+            nc.vector.tensor_tensor(out=results[g][h][:, lo:hi], in0=sums(g, U, h, ready, lo, hi), in1=gates[g][h][:, lo:hi], op=ALU.mult)
+            nc.sync.dma_start(out=out[g, HALF * h : HALF * (h + 1), lo:hi], in_=results[g][h][:, lo:hi])
 
-        vcopy, scopy = nc.vector.tensor_copy, nc.scalar.copy
-        sync, scalar = nc.sync, nc.scalar
+        vector_copy, scalar_copy = nc.vector.tensor_copy, nc.scalar.copy
 
-        nc.vector.memset(planes[W][:].bitcast(I32), 0)
-        nc.vector.memset(planes[U][:].bitcast(I32), 0)
+        for plane in planes:
+            nc.vector.memset(plane[:].bitcast(I32), 0)
         nc.vector.memset(bias_rows[:], 0.0)
         nc.vector.memset(codes[:, FIRST:PAD], 0)
         nc.vector.memset(scales[:, FIRST:PAD].bitcast(I32), 0)
 
-        first = load_x(0, 128)
-        second = load_x(128, 256)
-        load_plane(W, w_scales, (2,), scalar)
-        load_plane(W, w_scales, (3,), sync)
+        first = load_x(0, FIRST)
+        second = load_x(FIRST, LEFT)
+        load_plane(W, w_scales, 2, nc.scalar)
+        load_plane(W, w_scales, 3, nc.sync)
         load_words(W, w_words)
-        load_plane(W, w_scales, (0,), sync)
-        load_plane(W, w_scales, (1,), sync)
-        right = load_x(256, 512)
+        for q in (0, 1):
+            load_plane(W, w_scales, q, nc.sync)
+        right = load_x(LEFT, N)
         load_bias()
         load_words(U, u_words)
-        load_plane(U, u_scales, (2,), sync)
-        load_plane(U, u_scales, (3,), sync)
-        load_plane(U, u_scales, (0,), sync)
-        load_plane(U, u_scales, (1,), sync)
-        interleave(vcopy, first, 0, 64)
-        interleave(vcopy, first, 64, 128)
-        quantize(0, 64)
-        quantize(64, 128)
-        interleave(scopy, second, 216, 256)
-        interleave(vcopy, second, 128, 192)
-        interleave(vcopy, second, 192, 216)
-        quantize(128, 192)
-        quantize(192, 256)
-        multiply(1, W, 0, 128, 0)
-        multiply(0, W, 0, 128, 0)
-        multiply(1, W, 0, 256, 1)
-        multiply(0, W, 0, 256, 1)
-        multiply(0, W, 1, 256, 2)
-        multiply(1, U, 0, 256, 2)
-        multiply(1, W, 1, 256, 3)
-        multiply(0, U, 0, 256, 3)
-        interleave(scopy, right, 448, 512)
-        interleave(scopy, right, 416, 448)
-        interleave(vcopy, right, 256, 320)
+        for q in (2, 3, 0, 1):
+            load_plane(U, u_scales, q, nc.sync)
+
+        for lo in (0, STEP):
+            interleave(vector_copy, first, lo, lo + STEP)
+        for lo in (0, STEP):
+            quantize(lo)
+        interleave(scalar_copy, second, SCALAR_FROM_LEFT, LEFT)
+        interleave(vector_copy, second, FIRST, FIRST + STEP)
+        interleave(vector_copy, second, FIRST + STEP, SCALAR_FROM_LEFT)
+        for lo in (FIRST, FIRST + STEP):
+            quantize(lo)
+
+        for ready in (FIRST, LEFT):
+            for g in (1, 0):
+                multiply(g, W, 0, ready)
+        for g in (0, 1):
+            multiply(g, W, 1, LEFT)
+            multiply(1 - g, U, 0, LEFT)
+
+        interleave(scalar_copy, right, N - STEP, N)
+        interleave(scalar_copy, right, SCALAR_FROM_RIGHT, N - STEP)
+        interleave(vector_copy, right, LEFT, LEFT + STEP)
         turn_bias()
-        interleave(vcopy, right, 320, 384)
-        interleave(vcopy, right, 384, 416)
-        quantize(256, 320)
-        quantize(448, 512)
-        quantize(320, 384)
-        quantize(384, 448)
-        activate(1, 0, 128, 0, 128)
-        activate(0, 0, 128, 0, 128)
-        activate(1, 0, 256, 128, 256)
-        activate(0, 0, 256, 128, 256)
-        activate(0, 1, 256, 0, 256)
-        gate_and_store(1, 0, 256, 0, 256)
-        activate(1, 1, 256, 0, 256)
-        gate_and_store(0, 0, 256, 0, 256)
-        multiply(0, U, 1, 512, 0)
-        multiply(1, W, 1, 512, 0)
-        multiply(1, U, 1, 512, 1)
-        multiply(0, W, 1, 512, 1)
-        gate_and_store(0, 1, 512, 0, 256)
-        activate(1, 1, 512, 256, 512)
-        activate(0, 1, 512, 256, 512)
-        multiply(0, W, 0, 512, 2)
-        multiply(1, W, 0, 512, 2)
-        multiply(1, U, 0, 512, 3)
-        multiply(0, U, 0, 512, 3)
-        gate_and_store(1, 1, 512, 0, 256)
-        gate_and_store(1, 1, 512, 256, 512)
-        gate_and_store(0, 1, 512, 256, 512)
-        activate(1, 0, 512, 256, 512)
-        activate(0, 0, 512, 256, 512)
-        gate_and_store(1, 0, 512, 256, 512)
-        gate_and_store(0, 0, 512, 256, 512)
+        interleave(vector_copy, right, LEFT + STEP, LEFT + 2 * STEP)
+        interleave(vector_copy, right, LEFT + 2 * STEP, SCALAR_FROM_RIGHT)
+        for lo in (LEFT, N - STEP, LEFT + STEP, LEFT + 2 * STEP):
+            quantize(lo)
+
+        for ready, lo in ((FIRST, 0), (LEFT, FIRST)):
+            for g in (1, 0):
+                activate(g, 0, ready, lo, ready)
+        for g in (0, 1):
+            activate(g, 1, LEFT, 0, LEFT)
+        for g in (1, 0):
+            gate_and_store(g, 0, LEFT, 0, LEFT)
+
+        for g in (1, 0):
+            multiply(g, W, 1, N)
+            multiply(1 - g, U, 1, N)
+        for g in (1, 0):
+            activate(g, 1, N, LEFT, N)
+        for g in (0, 1):
+            gate_and_store(g, 1, N, 0, LEFT)
+
+        for k in (W, U):
+            for g in (1, 0):
+                multiply(g, k, 0, N)
+        for g in (1, 0):
+            gate_and_store(g, 1, N, LEFT, N)
+        for g in (1, 0):
+            activate(g, 0, N, LEFT, N)
+        for g in (1, 0):
+            gate_and_store(g, 0, N, LEFT, N)

@@ -167,9 +167,9 @@ def tile_rows_gglu_tanh_bias_kernel(tc, x, w_words, w_scales, u_words, u_scales,
         for g in (1, 0):
             gate_and_store(g, 0, LEFT, 0, LEFT)
 
-        for g in (1, 0):
-            multiply(g, W, 1, N)
-            multiply(1 - g, U, 1, N)
+        for g in (0, 1):
+            multiply(g, U, 1, N)
+            multiply(1 - g, W, 1, N)
         for g in (1, 0):
             activate(g, 1, N, LEFT, N)
         for g in (0, 1):

@@ -117,8 +117,8 @@ def tile_rows_gglu_tanh_bias_kernel(tc, x, w_words, w_scales, u_words, u_scales,
         for plane in planes:
             nc.vector.memset(plane[:].bitcast(I32), 0)
         nc.vector.memset(bias_rows[:], 0.0)
-        nc.vector.memset(codes[:, FIRST:PAD], 0)
-        nc.vector.memset(scales[:, FIRST:PAD].bitcast(I32), 0)
+        nc.vector.memset(codes[:, 64:PAD], 0)
+        nc.vector.memset(scales[:, 64:PAD].bitcast(I32), 0)
 
         first = load_x(0, FIRST)
         second = load_x(FIRST, LEFT)
@@ -133,40 +133,38 @@ def tile_rows_gglu_tanh_bias_kernel(tc, x, w_words, w_scales, u_words, u_scales,
         for q in (2, 3, 0, 1):
             load_plane(U, u_scales, q, nc.sync)
 
-        for lo in (0, STEP):
-            interleave(vector_copy, first, lo, lo + STEP)
-        for lo in (0, STEP):
-            quantize(lo)
-        interleave(scalar_copy, second, SCALAR_FROM_LEFT, LEFT)
-        interleave(vector_copy, second, FIRST, FIRST + STEP)
-        interleave(vector_copy, second, FIRST + STEP, SCALAR_FROM_LEFT)
-        for lo in (FIRST, FIRST + STEP):
-            quantize(lo)
-
-        for ready in (FIRST, LEFT):
-            for g in (1, 0):
-                multiply(g, W, 0, ready)
-        for g in (0, 1):
-            multiply(g, W, 1, LEFT)
-            multiply(1 - g, U, 0, LEFT)
-
-        interleave(scalar_copy, right, N - STEP, N)
-        interleave(scalar_copy, right, SCALAR_FROM_RIGHT, N - STEP)
-        interleave(vector_copy, right, LEFT, LEFT + STEP)
+        interleave(vector_copy, first, 0, 64)
+        interleave(vector_copy, first, 64, 128)
+        quantize(0)
+        interleave(scalar_copy, second, 192, 256)
+        interleave(vector_copy, second, 128, 192)
+        quantize(64)
+        quantize(128)
+        quantize(192)
+        multiply(1, W, 0, 64)
+        multiply(0, W, 0, 64)
+        multiply(1, W, 0, 256)
+        multiply(0, W, 0, 256)
+        multiply(0, W, 1, 256)
+        multiply(1, U, 0, 256)
+        multiply(1, W, 1, 256)
+        multiply(0, U, 0, 256)
+        interleave(scalar_copy, right, 448, 512)
+        interleave(scalar_copy, right, 416, 448)
         turn_bias()
-        interleave(vector_copy, right, LEFT + STEP, LEFT + 2 * STEP)
-        interleave(vector_copy, right, LEFT + 2 * STEP, SCALAR_FROM_RIGHT)
-        for lo in (LEFT, N - STEP, LEFT + STEP, LEFT + 2 * STEP):
+        interleave(vector_copy, right, 256, 320)
+        interleave(vector_copy, right, 320, 384)
+        interleave(vector_copy, right, 384, 416)
+        for lo in (256, 448, 320, 384):
             quantize(lo)
-
-        for ready, lo in ((FIRST, 0), (LEFT, FIRST)):
-            for g in (1, 0):
-                activate(g, 0, ready, lo, ready)
-        for g in (0, 1):
-            activate(g, 1, LEFT, 0, LEFT)
+        activate(1, 0, 64, 0, 64)
+        activate(1, 0, 256, 64, 256)
+        activate(0, 0, 64, 0, 64)
+        activate(0, 0, 256, 64, 256)
+        activate(0, 1, 256, 0, 256)
+        activate(1, 1, 256, 0, 256)
         for g in (1, 0):
             gate_and_store(g, 0, LEFT, 0, LEFT)
-
         for g in (0, 1):
             multiply(g, U, 1, N)
             multiply(1 - g, W, 1, N)
@@ -174,13 +172,14 @@ def tile_rows_gglu_tanh_bias_kernel(tc, x, w_words, w_scales, u_words, u_scales,
             activate(g, 1, N, LEFT, N)
         for g in (0, 1):
             gate_and_store(g, 1, N, 0, LEFT)
-
         for k in (W, U):
             for g in (1, 0):
                 multiply(g, k, 0, N)
         for g in (1, 0):
             gate_and_store(g, 1, N, LEFT, N)
-        for g in (1, 0):
-            activate(g, 0, N, LEFT, N)
-        for g in (1, 0):
-            gate_and_store(g, 0, N, LEFT, N)
+        activate(1, 0, 512, 256, 512)
+        activate(0, 0, 512, 256, 384)
+        activate(0, 0, 512, 384, 512)
+        gate_and_store(1, 0, 512, 256, 512)
+        gate_and_store(0, 0, 512, 256, 384)
+        gate_and_store(0, 0, 512, 384, 512)

@@ -24,6 +24,7 @@ HALVES = M // HALF
 W, U = 0, 1
 BANKS = 4
 RUN = 4
+BIAS_STEP = QUADRANT // (G * HALVES)
 ALIGN = 256
 
 FIRST = 128
@@ -45,8 +46,8 @@ def tile_rows_gglu_tanh_bias_kernel(tc, x, w_words, w_scales, u_words, u_scales,
 
         words = [keep.tile([P, 2 * M], U8, align_bytes=ALIGN, name=f"words{k}") for k in (W, U)]
         planes = [keep.tile([P, M], U8, align_bytes=ALIGN, name=f"plane{k}") for k in (W, U)]
-        bias_rows = keep.tile([P, G * HALVES, QUADRANT], F32, align_bytes=ALIGN)
-        bias = keep.tile([P, G * HALVES, QUADRANT], F32, align_bytes=ALIGN)
+        bias_rows = keep.tile([P, QUADRANT], F32, align_bytes=ALIGN)
+        bias = keep.tile([P, QUADRANT], F32, align_bytes=ALIGN)
         grouped = keep.tile([P, N, PACK], BF16, align_bytes=ALIGN)
         codes = keep.tile([P, PAD + N], U32, align_bytes=ALIGN)
         scales = keep.tile([P, PAD + N], U8, align_bytes=ALIGN)
@@ -68,10 +69,10 @@ def tile_rows_gglu_tanh_bias_kernel(tc, x, w_words, w_scales, u_words, u_scales,
             queue.dma_start(out=planes[k][QUADRANT * q : QUADRANT * q + 4, :].bitcast(I32), in_=rows[4 * q : 4 * q + 4, :])
 
         def load_bias():
-            nc.sync.dma_start(out=bias_rows[0:P:QUADRANT, :, :], in_=b.rearrange("g (h q j) o -> q (g h) (j o)", q=4, j=QUADRANT))
+            nc.sync.dma_start(out=bias_rows[0:P:BIAS_STEP, :], in_=b.rearrange("g (h q j) o -> q (g h) (j o)", q=4, j=QUADRANT))
 
         def turn_bias():
-            nc.vector.transpose(out=bias[:].rearrange("p c j -> p (c j)"), in_=bias_rows[:].rearrange("p c j -> p (c j)"))
+            nc.vector.transpose(out=bias[:], in_=bias_rows[:])
 
         def interleave(copy, chunk, lo, hi):
             raw, start = chunk
@@ -106,7 +107,8 @@ def tile_rows_gglu_tanh_bias_kernel(tc, x, w_words, w_scales, u_words, u_scales,
             return bank[:, lo + N - ready : hi + N - ready]
 
         def activate(g, h, ready, lo, hi):
-            nc.scalar.activation(out=gates[g][h][:, lo:hi], in_=sums(g, W, h, ready, lo, hi), func=ACT.Tanh, bias=bias[:, g * HALVES + h, 0:1])
+            column = BIAS_STEP * (g * HALVES + h)
+            nc.scalar.activation(out=gates[g][h][:, lo:hi], in_=sums(g, W, h, ready, lo, hi), func=ACT.Tanh, bias=bias[:, column : column + 1])
 
         def gate_and_store(g, h, ready, lo, hi):
             nc.vector.tensor_tensor(out=results[g][h][:, lo:hi], in0=sums(g, U, h, ready, lo, hi), in1=gates[g][h][:, lo:hi], op=ALU.mult)
@@ -150,11 +152,11 @@ def tile_rows_gglu_tanh_bias_kernel(tc, x, w_words, w_scales, u_words, u_scales,
         multiply(1, W, 1, 256)
         multiply(0, U, 0, 256)
         interleave(scalar_copy, right, 448, 512)
-        interleave(scalar_copy, right, 416, 448)
+        interleave(scalar_copy, right, 408, 448)
         turn_bias()
         interleave(vector_copy, right, 256, 320)
         interleave(vector_copy, right, 320, 384)
-        interleave(vector_copy, right, 384, 416)
+        interleave(vector_copy, right, 384, 408)
         for lo in (256, 448, 320, 384):
             quantize(lo)
         activate(1, 0, 64, 0, 64)

@@ -123,23 +123,26 @@ def tile_rows_gglu_tanh_bias_kernel(tc, x, w_words, w_scales, u_words, u_scales,
         nc.vector.memset(scales[:, 64:PAD].bitcast(I32), 0)
 
         first = load_x(0, FIRST)
-        second = load_x(FIRST, LEFT)
         load_plane(W, w_scales, 2, nc.scalar)
         load_plane(W, w_scales, 3, nc.sync)
+        second = load_x(FIRST, LEFT)
         load_words(W, w_words)
-        for q in (0, 1):
-            load_plane(W, w_scales, q, nc.sync)
+        load_plane(W, w_scales, 0, nc.sync)
+        load_plane(W, w_scales, 1, nc.sync)
         right = load_x(LEFT, N)
         load_bias()
         load_words(U, u_words)
-        for q in (2, 3, 0, 1):
-            load_plane(U, u_scales, q, nc.sync)
+        load_plane(U, u_scales, 2, nc.sync)
+        load_plane(U, u_scales, 3, nc.sync)
+        load_plane(U, u_scales, 0, nc.sync)
+        load_plane(U, u_scales, 1, nc.sync)
 
         interleave(vector_copy, first, 0, 64)
         interleave(vector_copy, first, 64, 128)
         quantize(0)
-        interleave(scalar_copy, second, 192, 256)
+        interleave(scalar_copy, second, 208, 256)
         interleave(vector_copy, second, 128, 192)
+        interleave(vector_copy, second, 192, 208)
         quantize(64)
         quantize(128)
         quantize(192)

@@ -25,6 +25,7 @@ W, U = 0, 1
 BANKS = 4
 RUN = 4
 BIAS_STEP = QUADRANT // (G * HALVES)
+PLANE_AT, SCALES_AT = 64, 128
 ALIGN = 256
 
 FIRST = 128
@@ -45,12 +46,12 @@ def tile_rows_gglu_tanh_bias_kernel(tc, x, w_words, w_scales, u_words, u_scales,
         ctx.enter_context(tc.manual_schedule())
 
         words = [keep.tile([P, 2 * M], U8, align_bytes=ALIGN, name=f"words{k}") for k in (W, U)]
-        planes = [keep.tile([P, M], U8, align_bytes=ALIGN, name=f"plane{k}") for k in (W, U)]
+        planes = [keep.tile([P, PLANE_AT + M], U8, align_bytes=ALIGN, name=f"plane{k}")[:, PLANE_AT:] for k in (W, U)]
         bias_rows = keep.tile([P, QUADRANT], F32, align_bytes=ALIGN)
         bias = keep.tile([P, QUADRANT], F32, align_bytes=ALIGN)
         grouped = keep.tile([P, N, PACK], BF16, align_bytes=ALIGN)
         codes = keep.tile([P, PAD + N], U32, align_bytes=ALIGN)
-        scales = keep.tile([P, PAD + N], U8, align_bytes=ALIGN)
+        scales = keep.tile([P, SCALES_AT + PAD + N], U8, align_bytes=ALIGN, name="scales")[:, SCALES_AT:]
         banks = [[psum.tile([HALF, N], F32, name=f"bank{g}{i}") for i in range(BANKS)] for g in range(G)]
         gates = [[keep.tile([P, N], F32, align_bytes=ALIGN, name=f"gate{g}{h}") for h in range(HALVES)] for g in range(G)]
         results = [[keep.tile([P, N], F32, align_bytes=ALIGN, name=f"result{g}{h}") for h in range(HALVES)] for g in range(G)]

from contextlib import ExitStack

import concourse.mybir as mybir

G, D, M, N = 2, 256, 256, 512
FLOPS = 2 * 2 * G * D * M * N

F32 = mybir.dt.float32
BF16 = mybir.dt.bfloat16
I32 = mybir.dt.int32
U32 = mybir.dt.uint32
U8 = mybir.dt.uint8
FP8X4 = mybir.dt.float8_e4m3fn_x4
FP4X4 = mybir.dt.float4_e2m1fn_x4
ACT = mybir.ActivationFunctionType
ALU = mybir.AluOpType

P = 128
QUADRANT = 32
PACK = 4
ROWS = D // PACK
HALF = 128
HALVES = M // HALF
W, U = 0, 1
BANKS = 4
RUN = 4
BIAS_STEP = QUADRANT // (G * HALVES)
PLANE_AT, SCALES_AT = 64, 128
ALIGN = 256

FIRST = 128
LEFT = 256
STEP = 64
PAD = N
SCALAR_FROM_LEFT = 216
SCALAR_FROM_RIGHT = 416


def tile_rows_gglu_tanh_bias_kernel(tc, x, w_words, w_scales, u_words, u_scales, b, out):
    nc = tc.nc
    x_rows = x.rearrange("g (p j) n -> (g p) j n", j=PACK)

    with ExitStack() as ctx:
        keep = ctx.enter_context(tc.tile_pool(name="keep", bufs=1))
        psum = ctx.enter_context(tc.psum_pool(name="psum", bufs=1))
        ctx.enter_context(tc.manual_schedule())

        words = [keep.tile([P, 2 * M], U8, align_bytes=ALIGN, name=f"words{k}") for k in (W, U)]
        planes = [keep.tile([P, PLANE_AT + M], U8, align_bytes=ALIGN, name=f"plane{k}")[:, PLANE_AT:] for k in (W, U)]
        bias_rows = keep.tile([P, QUADRANT], F32, align_bytes=ALIGN)
        bias = keep.tile([P, QUADRANT], F32, align_bytes=ALIGN)
        grouped = keep.tile([P, N, PACK], BF16, align_bytes=ALIGN)
        codes = keep.tile([P, PAD + N], U32, align_bytes=ALIGN)
        scales = keep.tile([P, SCALES_AT + PAD + N], U8, align_bytes=ALIGN, name="scales")[:, SCALES_AT:]
        banks = [[psum.tile([HALF, N], F32, name=f"bank{g}{i}") for i in range(BANKS)] for g in range(G)]
        gates = [[keep.tile([P, N], F32, align_bytes=ALIGN, name=f"gate{g}{h}") for h in range(HALVES)] for g in range(G)]
        results = [[keep.tile([P, N], F32, align_bytes=ALIGN, name=f"result{g}{h}") for h in range(HALVES)] for g in range(G)]
        passes = [[] for g in range(G)]

        def load_x(lo, hi):
            raw = keep.tile([P, PACK, hi - lo], F32, align_bytes=ALIGN, name=f"raw{lo}")
            nc.sync.dma_start(out=raw[:], in_=x_rows[:, :, lo:hi])
            return raw, lo

        def load_words(k, source):
            nc.sync.dma_start(out=words[k][:].bitcast(I32), in_=source.rearrange("g p c -> (g p) c").bitcast(I32))

        def load_plane(k, source, q, queue):
            rows = source.rearrange("g f m -> (g f) m").bitcast(I32)
            queue.dma_start(out=planes[k][QUADRANT * q : QUADRANT * q + 4, :].bitcast(I32), in_=rows[4 * q : 4 * q + 4, :])

        def load_bias():
            nc.sync.dma_start(out=bias_rows[0:P:BIAS_STEP, :], in_=b.rearrange("g (h q j) o -> q (g h) (j o)", q=4, j=QUADRANT))

        def turn_bias():
            nc.vector.transpose(out=bias[:], in_=bias_rows[:])

        def interleave(copy, chunk, lo, hi):
            raw, start = chunk
            copy(
                out=grouped[:, lo:hi, :].rearrange("p (c i) j -> p c j i", i=RUN),
                in_=raw[:, :, lo - start : hi - start].rearrange("p j (c i) -> p c j i", i=RUN),
            )

        def quantize(lo):
            nc.vector.quantize_mx(
                out=codes[:, PAD + lo : PAD + lo + STEP].bitcast(FP8X4),
                scales=scales[:, PAD + lo : PAD + lo + STEP],
                in_=grouped[:, lo : lo + STEP, :].rearrange("p n j -> p (n j)"),
            )

        def multiply(g, k, h, ready):
            rows = slice(ROWS * g, ROWS * (g + 1))
            window = slice(PAD + ready - N, PAD + ready)
            nc.tensor.matmul_mx(
                out=banks[g][len(passes[g]) % BANKS][:],
                lhsT=words[k][rows, 2 * HALF * h : 2 * HALF * (h + 1)].bitcast(FP4X4),
                lhsT_scale=planes[k][rows, HALF * h : HALF * (h + 1)],
                rhs=codes[rows, window].bitcast(FP8X4),
                rhs_scale=scales[rows, window],
                start=True,
                stop=True,
            )
            passes[g].append((k, h, ready))

        def sums(g, k, h, ready, lo, hi):
            bank = banks[g][passes[g].index((k, h, ready)) % BANKS]
            return bank[:, lo + N - ready : hi + N - ready]

        def activate(g, h, ready, lo, hi):
            column = BIAS_STEP * (g * HALVES + h)
            nc.scalar.activation(out=gates[g][h][:, lo:hi], in_=sums(g, W, h, ready, lo, hi), func=ACT.Tanh, bias=bias[:, column : column + 1])

        def gate_and_store(g, h, ready, lo, hi):
            nc.vector.tensor_tensor(out=results[g][h][:, lo:hi], in0=sums(g, U, h, ready, lo, hi), in1=gates[g][h][:, lo:hi], op=ALU.mult)
            nc.sync.dma_start(out=out[g, HALF * h : HALF * (h + 1), lo:hi], in_=results[g][h][:, lo:hi])

        vector_copy, scalar_copy = nc.vector.tensor_copy, nc.scalar.copy

        for plane in planes:
            nc.vector.memset(plane[:].bitcast(I32), 0)
        nc.vector.memset(bias_rows[:], 0.0)
        nc.vector.memset(codes[:, 64:PAD], 0)
        nc.vector.memset(scales[:, 64:PAD].bitcast(I32), 0)

        first = load_x(0, FIRST)
        load_plane(W, w_scales, 2, nc.scalar)
        load_plane(W, w_scales, 3, nc.sync)
        second = load_x(FIRST, LEFT)
        load_words(W, w_words)
        load_plane(W, w_scales, 0, nc.sync)
        load_plane(W, w_scales, 1, nc.sync)
        right = load_x(LEFT, N)
        load_bias()
        load_words(U, u_words)
        load_plane(U, u_scales, 2, nc.sync)
        load_plane(U, u_scales, 3, nc.sync)
        load_plane(U, u_scales, 0, nc.sync)
        load_plane(U, u_scales, 1, nc.sync)

        interleave(vector_copy, first, 0, 64)
        interleave(vector_copy, first, 64, 128)
        quantize(0)
        interleave(scalar_copy, second, 208, 256)
        interleave(vector_copy, second, 128, 192)
        interleave(vector_copy, second, 192, 208)
        quantize(64)
        quantize(128)
        quantize(192)
        multiply(1, W, 0, 64)
        multiply(0, W, 0, 64)
        multiply(1, W, 0, 256)
        multiply(0, W, 0, 256)
        multiply(0, W, 1, 256)
        multiply(1, U, 0, 256)
        multiply(1, W, 1, 256)
        multiply(0, U, 0, 256)
        interleave(scalar_copy, right, 448, 512)
        interleave(scalar_copy, right, 408, 448)
        turn_bias()
        interleave(vector_copy, right, 256, 320)
        interleave(vector_copy, right, 320, 384)
        interleave(vector_copy, right, 384, 408)
        for lo in (256, 448, 320, 384):
            quantize(lo)
        activate(1, 0, 64, 0, 64)
        activate(1, 0, 256, 64, 256)
        activate(0, 0, 64, 0, 64)
        activate(0, 0, 256, 64, 256)
        activate(0, 1, 256, 0, 256)
        activate(1, 1, 256, 0, 256)
        for g in (1, 0):
            gate_and_store(g, 0, LEFT, 0, LEFT)
        for g in (0, 1):
            multiply(g, U, 1, N)
            multiply(1 - g, W, 1, N)
        for g in (1, 0):
            activate(g, 1, N, LEFT, N)
        for g in (0, 1):
            gate_and_store(g, 1, N, 0, LEFT)
        for k in (W, U):
            for g in (1, 0):
                multiply(g, k, 0, N)
        for g in (1, 0):
            gate_and_store(g, 1, N, LEFT, N)
        activate(1, 0, 512, 256, 512)
        activate(0, 0, 512, 256, 384)
        activate(0, 0, 512, 384, 512)
        gate_and_store(1, 0, 512, 256, 512)
        gate_and_store(0, 0, 512, 256, 384)
        gate_and_store(0, 0, 512, 384, 512)
